import numpy as np, ml_dtypes
CORES = [16,17,18,19,32,33,34,35]
N = 8
BF = ml_dtypes.bfloat16
def gentries(a):
    return np.ascontiguousarray(a.reshape(8, 16, -1).transpose(0, 2, 1)).reshape(8, -1)
def gtable(e):
    e = np.asarray(e); return np.ascontiguousarray(e.reshape(8, -1, 16).transpose(0, 2, 1)).reshape(128, -1).astype(np.int32)
W, V, I, RO = 2048, 2048, 128, 3
P = V // I
def parts(rng):
    return (rng.integers(0, W, (N, 8, 16, W)), rng.integers(0, 256, (N, 8, 16, V)), rng.integers(0, 256, (N, 8, 16, I)),
            rng.integers(0, W, (N, 8, I)), rng.integers(0, 256, (N, 8, 16)))
def pack(S, X, x, s, w):
    return {"stm": np.ascontiguousarray(S.reshape(N, 128, W)).astype(np.int32), "vx": X.reshape(N, 128, V).astype(np.float32).astype(BF),
            "x0": x.reshape(N, 128, I).astype(np.float32).astype(BF), "s0": np.stack([gtable(a) for a in s]), "wt": w.reshape(N, 128, 1).astype(np.int32)}
def two(rng, lo, hi, shape):
    return np.where(rng.random(shape) < 0.5, lo, hi)
def tame(rng, S, w, cl):
    col = np.arange(W); ev = col[((col >> 4) & 1) == 0]
    off = np.where(cl, 0, rng.integers(1, 16, cl.shape))
    S[:, ev] = 32 * np.argsort(rng.random((16, W // 32, 16)), axis=1).reshape(16, W // 2) + 16 + ((ev + off) & 15)
    w[:] = 32 * rng.integers(1, 8, 16)
    return ev
def lay(rng, S, w, cl, no):
    off = rng.integers(1, 15, cl.shape); off = np.where(cl, 0, off + (off >= 16 - no))
    S[:] = 16 * rng.integers(0, W // 16, cl.shape) + ((np.arange(W) + off) & 15)
    w[:] = 32 * rng.integers(1, 8, 16)
def wake(S, X, w, k, c):
    if (S[k, c] & (V - 1)) == (S[k ^ 1, c] & (V - 1)): S[k ^ 1, c] = S[k ^ 1, c] ^ 16
    a = S[k, c] & (V - 1); b = S[k ^ 1, c] & (V - 1)
    X[0, b] = X[0, a] ^ 1
    if int(np.add.reduce(w * np.abs(X[:, a] - X[:, b]))) & (W - 1) == 0: w[0] = w[0] ^ 32
def setup_inputs(rng):
    return pack(*parts(rng))
def setup_inputs_corners(rng):
    S, X, x, s, w = parts(rng); M = W // 2; role = rng.permutation(N)
    for q in range(N):
        kinds = rng.permutation(8); gx = int(rng.integers(0, 8))
        for g in range(8):
            kind = int(kinds[g])
            if role[q] == 0 or role[q] == 2: kind = 0 if g % 2 == 0 else 2
            if role[q] == 1: kind = 1
            if role[q] == 2 and g == gx: kind = 8
            if kind == 6:
                S[q, g] = np.arange(W)[None, :]; s[q, g, 0] = W - 1; s[q, g, I - 1] = 0; continue
            if kind == 7:
                s[q, g] = two(rng, 0, W - 1, I); continue
            cl = np.zeros((16, M), bool); p = rng.permutation(M)
            if kind == 1: cl[:] = True
            if kind == 2: cl[15] = True
            if kind == 3: cl[0] = True; cl[15] = True
            if kind == 4: cl[14:] = rng.random(M) < 0.5
            if kind == 5: cl = np.argsort(rng.random((16, M)), axis=0) < rng.integers(0, 17, M)
            if kind == 8:
                n = int(rng.integers(15, 18)); cl[3, p[:n]] = True; cl[9, p[:n]] = True
            ev = tame(rng, S[q, g], w[q, g], cl)
            s[q, g] = rng.permutation(ev[p[:I]])
    return pack(S, X, x, s, w)
def setup_inputs_late(rng):
    S, X, x, s, w = parts(rng); odd = int(rng.integers(0, 2)); col = np.arange(W)
    for q in range(N):
        if q % 2 == odd:
            al = int(rng.integers(1, 16)); n = 16 * int(rng.integers(I // 16, 5 * I // 16)) + al
            fk = rng.permutation(8 * (I - 1)).reshape(8, I - 1) < n
            for g in range(8):
                m = np.where((col & 1) == 1, rng.integers(0, 2, W), rng.integers(2, 5, W)); m[W - 1] = 0
                lay(rng, S[q, g], w[q, g], np.argsort(rng.random((16, W)), axis=0) < m, al)
                s[q, g] = 2 * rng.integers(0, W // 2, I) + 1; s[q, g, :I - 1] -= fk[g].astype(np.int64); s[q, g, I - 1] = W - 1
            continue
        kinds = rng.permutation(8)
        for g in range(8):
            kind = int(kinds[g]) // 2; Sg, Xg, wg = S[q, g], X[q, g], w[q, g]
            if kind == 3: continue
            no = int(rng.integers(1, 16)); e = 16 * (1 + rng.permutation(W // 16 - 1)[:4])
            if kind == 0:
                lay(rng, Sg, wg, np.zeros((16, W), bool), no)
                k = int(rng.integers(0, 16)); c = int(rng.integers(0, W)); at = np.arange(c & 15, W, 16)
                Sg[k, at] = c; s[q, g] = rng.choice(at, I); wake(Sg, Xg, wg, k, c); continue
            lay(rng, Sg, wg, rng.random((16, W)) < 0.0625, no)
            if kind == 1:
                Sg[Sg == 0] = 16
                Sg[0, e[0]] = 0; Sg[0, e[1]] = 5; Sg[1, e[1]] = 0
                s[q, g, 0] = e[0]; s[q, g, 1] = e[1]; wake(Sg, Xg, wg, 0, 0)
            if kind == 2:
                ka = int(rng.integers(0, 15)); kb = int(rng.integers(ka + 1, 16))
                Sg[:, e] = 16 * rng.integers(0, W // 16, (16, 4)) + rng.integers(1, 16, (16, 4))
                Sg[ka, e] = 16 * rng.integers(1, W // 16, 4); Sg[kb, e] = 0
                z = np.abs(Xg[:, Sg[kb, 0] & (V - 1)] - Xg[:, Sg[kb ^ 1, 0] & (V - 1)])
                s[q, g, 1::2] = rng.choice(e, I // 2); x[q, g, :, 1::2] = z[:, None]
    return pack(S, X, x, s, w)
def setup_inputs_ties(rng):
    S, X, x, s, w = parts(rng)
    pool = np.argsort(rng.random((N, 8, W)), axis=-1)[..., :32]; pool[..., 0] = W - 1; pool[..., 1] = 0
    S = np.take_along_axis(pool[:, :, None, :], rng.integers(0, 32, (N, 8, 16, W)), 3)
    s = np.take_along_axis(pool, rng.integers(0, 32, (N, 8, I)), 2)
    few = np.take_along_axis(X[..., :5], rng.integers(0, 5, (N, 8, 1, V)), 3)
    X[:, ::2] = few[:, ::2]; x[:, 1::2] = x[:, 1::2, :, :1]
    return pack(S, X, x, s, w)
def setup_inputs_ends(rng):
    S, X, x, s, w = parts(rng)
    S = np.where(rng.random(S.shape) < 0.7, two(rng, 0, W - 1, S.shape), S)
    S[..., 0] = two(rng, 0, W - 1, (N, 8, 16)); S[..., W - 1] = two(rng, 0, W - 1, (N, 8, 16))
    S[:, :, [0, 1, 14, 15], 0] = np.array([0, W - 1, 0, W - 1]); S[:, :, [0, 1, 14, 15], W - 1] = np.array([0, W - 1, W - 1, 0])
    S[:, :, 4:6, 0] = 0; S[:, :, 4:6, W - 1] = W - 1
    q = 16 * rng.integers(1, W // 16 - 1, (N, 8)); S[:, :, 2, 0] = q; S[:, :, 2, W - 1] = q + 15
    for a in range(N):
        for g in range(8):
            S[a, g, 2:4, q[a, g]] = W - 1; S[a, g, 2:4, q[a, g] + 15] = 0
    S[:, :, 1, W - 2] = W - 1; S[:, :, 15, W - 2] = W - 1
    X = two(rng, 0, 255, X.shape); X[..., 0] = 0; X[..., V - 1] = 255
    x = two(rng, 0, 255, x.shape); w = two(rng, 0, 255, w.shape)
    w[:, 0] = 255; w[:, 7] = 255; w[:, 1::5] = 0; w[:, 1::5, 15] = 255; w[:, 1::5, 14] = 2
    s = np.where(rng.random(s.shape) < 0.8, two(rng, 0, W - 1, s.shape), s); s[N - 1] = two(rng, 0, W - 1, (8, I))
    s[:, 7, I - 1] = W - 1; s[:, 0, 2] = W - 1; s[:, 7, 1] = 0
    s[:, 1::5, 3] = W - 2; s[:, 1::5, I - 1] = W - 2; s[:, 1::5, I - 2] = W - 1; s[:, 1::5, 4] = W - 1
    return pack(S, X, x, s, w)
def setup_inputs_spread(rng):
    S, X, x, s, w = parts(rng)
    p = rng.choice(np.array([1.0, 1.5, 2.0, 4.0]), (N, 8, 1, 1)); fl = rng.random((N, 8, 1, 1)) < 0.5
    S = np.minimum((W * rng.random(S.shape) ** p).astype(np.int64), W - 1); S = np.where(fl, W - 1 - S, S)
    s = np.minimum((W * rng.random(s.shape) ** p[..., 0]).astype(np.int64), W - 1)
    X = np.minimum((np.exp2(8 * rng.random((N, 8, 1, V))) * rng.random(X.shape)).astype(np.int64), 255)
    x = np.minimum((np.exp2(8 * rng.random((N, 8, 1, I))) * rng.random(x.shape)).astype(np.int64), 255)
    w = np.minimum(np.exp2(8 * rng.random(w.shape)).astype(np.int64), 255)
    return pack(S, X, x, s, w)
def check_inputs(d):
    bad = []
    for k, lo, hi in (("stm", 0, W - 1), ("vx", 0, 255), ("x0", 0, 255), ("s0", 0, W - 1), ("wt", 0, 255)):
        v = np.asarray(d[k]).astype(np.float64)
        if not (np.min(v) >= lo and np.max(v) <= hi): bad.append("range of " + k)
        elif np.any(v != np.floor(v)): bad.append("whole numbers in " + k)
    return bad
def reference(stm, vx, x0, s0, wt):
    S = stm.astype(np.int64).reshape(N, 8, 16, W); X = vx.astype(np.float32).astype(np.int64).reshape(N, 8, 16, V)
    x = x0.astype(np.float32).astype(np.int64).reshape(N, 8, 16, I); w = wt.astype(np.int64).reshape(N, 8, 16, 1, 1)
    s = np.stack([gentries(a) for a in s0]).astype(np.int64)
    A = np.zeros(N, np.int64); mate = np.arange(16) ^ 1
    for t in range(RO):
        c = np.take_along_axis(S, s[:, :, None, :], 3)
        a = np.take_along_axis(S, c, 3) & (V - 1); b = np.take_along_axis(S[:, :, mate], c, 3) & (V - 1)
        z = np.abs(np.take_along_axis(X, a.reshape(N, 8, 1, 16 * I), 3) - np.take_along_axis(X, b.reshape(N, 8, 1, 16 * I), 3)).reshape(N, 8, 16, 16, I)
        u = np.add.reduce(w * z, axis=2) & (W - 1)
        claim = ((((u * u) >> 5) + u + c + A[:, None, None, None]) & 15) == (s & 15)[:, :, None, :]
        n = np.add.accumulate(claim.astype(np.int64), axis=2)
        has = n[:, :, 15] >= 1; fork = n[:, :, 15] >= 2
        k1 = np.argmax(claim & (n == 1), axis=2); k2 = np.argmax(claim & (n == 2), axis=2)
        c1 = np.take_along_axis(c, k1[:, :, None, :], 2)[:, :, 0]; c2 = np.take_along_axis(c, k2[:, :, None, :], 2)[:, :, 0]
        u1 = np.take_along_axis(u, k1[:, :, None, :], 2)[:, :, 0]
        z1 = np.take_along_axis(z, k1[:, :, None, None, :], 3)[:, :, :, 0]; z2 = np.take_along_axis(z, k2[:, :, None, None, :], 3)[:, :, :, 0]
        h = 1 + t % (N - 1)
        came = np.roll(fork, h, axis=0); cc = np.roll(c2, h, axis=0); cx = np.roll(np.abs(x - z2), h, axis=0)
        s = np.where(has, c1, np.where(came, cc, (5 * s + u[:, :, 0]) & (W - 1)))
        x = np.where(has[:, :, None], (x + z1) >> 1, np.where(came[:, :, None], cx, x))
        for r in range(N):
            for g in range(8):
                i = np.flatnonzero(has[r, g])
                X[r, g][:, P * i + (u1[r, g, i] & (P - 1))] = z1[r, g][:, i]
                col, at = np.unique(c1[r, g, i], return_index=True)
                i = i[at]; k = k1[r, g, i]
                S[r, g, k, col] = (S[r, g, k, col] + u1[r, g, i]) & (W - 1)
        A = np.add.reduce(fork.astype(np.int64), axis=(1, 2)) & 15
    return {"yt": np.add.reduce(S.reshape(N, 128, W // 256, 256), axis=2).astype(np.float32), "yv": X.reshape(N, 128, V).astype(np.float32).astype(BF),
            "yx": x.reshape(N, 128, I).astype(np.float32).astype(BF), "ys": np.stack([gtable(e) for e in s]).astype(np.float32)}

@@ -1,0 +1,532 @@
+import math
+from concourse.mybir import AluOpType as OP, ActivationFunctionType as AF
+
+N, RO = 8, 3
+NENG = 8
+CH = 32
+
+F32, F16, BF, I4, U2 = "float32", "float16", "bfloat16", "int32", "uint16"
+SCRATCH = {}
+
+
+def _sb(dtype, **bufs):
+    for name in bufs:
+        SCRATCH[name] = ("sbuf", [128, bufs[name]], dtype)
+
+
+_sb(I4, S=2176, si=8, wi=1)
+_sb(BF, ZX=4096, xb=128)
+_sb(U2, su=8)
+_sb(I4, cp=1, cq=4)
+_sb(F32, cI=144, cf=16, tq=128, rc=128, blk=128, mk=128, l256=16, rm=16, gm=8, ex=16, z16=16, THR=128, IL=8, XO=8, on32=128, il0=8)
+_sb(F16, I16=128, P16=128, I32=128, L1=144, LK=144, DA=2048, DB=2048, BM=2048, BN=128, SEL=1024, on16=128, TQ=128, RC=128,
+    BO=128, BF1=128, BF2=128, RQ=8, GI=8, CT=16)
+_sb(BF, IB=128, NIB=128, WT=144, VJ=16)
+_sb(U2, Cu=128, ABT=256, ou=16, c1u=8, sou=8, xou=8)
+_sb(F16, C16=128, G0=1024, G1=1024, sA=8, cl=128, ukf=128, FS=256, F1X=384, F2=128, lt=128, c1h=8)
+_sb(BF, XB=2048, DD=2048, EQ=1024, z1=128, z2=128, sg=8)
+_sb(I4, ui=128, w2=128, sq=128, y=128, yy=128, uk=128, Sc=128, Sd=128, Sn=128, x1=8, x2=8, x3=8, n2=8, n3=8, se=8, xv=128,
+    xba=128, xm=128, xn=128)
+_sb(F32, so=8, n1=8, h1=8, h2=8, sb=8, fc=1, x256=128, sf=8, yto=256)
+SEMAPHORES = ["qv", "qs", "qp", "qg", "dS0", "dX", "dx0", "dw", "ds0", "oV", "oT", "oX", "oS", "sent"]
+for _t in range(RO):
+    _sb(F32, **{"mN%d" % _t: 8, "rN%d" % _t: 8})
+    _sb(BF, **{"mX%d" % _t: 128, "rX%d" % _t: 128})
+    SEMAPHORES += ["aN%d" % _t, "aX%d" % _t]
+PSUM = ["b%d" % _b for _b in range(8)]
+for _b in PSUM:
+    SCRATCH[_b] = ("psum", [128, 512], F32)
+
+
+def make_tracker(g, T):
+    eng = {"v": g.vector, "s": g.scalar, "p": g.tensor, "g": g, "y": g.sync}
+    sem = {"v": "qv", "s": "qs", "p": "qp", "g": "qg"}
+    count = {}
+    clock = dict((q, {}) for q in eng)
+    event = {}
+    hist = {}
+
+    def deps(q, rd, wr):
+        need = {}
+        for acc, isw in ((rd, False), (wr, True)):
+            for name, a, b in acc:
+                for (a0, b0, w0, src, n) in hist.get(name, []):
+                    if name in PSUM:
+                        hit = (src != q) or (q != "p" and a < b0 and a0 < b and (isw or w0))
+                    else:
+                        hit = a < b0 and a0 < b and (isw or w0)
+                    if hit and n > clock[q].get(src, 0):
+                        need[src] = max(need.get(src, 0), n)
+        return need
+
+    def wait(q, need):
+        for src in sorted(need):
+            n = need[src]
+            if any(event[(o, need[o])].get(src, 0) >= n for o in need if o != src):
+                continue
+            eng[q].wait_ge(T.sem[sem.get(src, src)], n)
+        for src in need:
+            for k, m in event[(src, need[src])].items():
+                clock[q][k] = max(clock[q].get(k, 0), m)
+
+    def note(src, n, q, rd, wr):
+        ev = dict(clock[q])
+        ev[src] = n
+        event[(src, n)] = ev
+        for name, a, b in wr:
+            keep = []
+            for h in hist.get(name, []):
+                if not (a <= h[0] and h[1] <= b and ev.get(h[3], 0) >= h[4]):
+                    keep.append(h)
+            hist[name] = keep + [(a, b, True, src, n)]
+        for name, a, b in rd:
+            keep = [h for h in hist.get(name, []) if h[2] or h[3] != src or not (a <= h[0] and h[1] <= b)]
+            hist[name] = keep + [(a, b, False, src, n)]
+
+    def rng(x):
+        return (x, 0, T[x].shape[1]) if isinstance(x, str) else x
+
+    def do(q, rd, wr, fn):
+        rd = [rng(x) for x in rd]
+        wr = [rng(x) for x in wr]
+        wait(q, deps(q, rd, wr))
+        n = count.get(q, 0) + 1
+        count[q] = n
+        fn(eng[q]).then_inc(T.sem[sem[q]], 1)
+        note(q, n, q, rd, wr)
+
+    def dma(q, s, rd, wr, out, in_):
+        rd = [rng(x) for x in rd]
+        wr = [rng(x) for x in wr]
+        wait(q, deps(q, rd, wr))
+        eng[q].dma_start(out, in_).then_inc(T.sem[s], 16)
+        note(s, 16, q, rd, wr)
+
+    def arrive(s, n, wr):
+        event[(s, n)] = {s: n}
+        for x in wr:
+            hist[x] = [rng(x)[1:] + (True, s, n)]
+
+    def ready(q, rd):
+        wait(q, deps(q, [rng(x) for x in rd], []))
+
+    def finish():
+        for q in ("v", "s", "p", "g"):
+            if count.get(q, 0) > clock["g"].get(q, 0):
+                wait("g", {q: count[q]})
+    return do, dma, arrive, ready, finish, wait
+
+
+def rank_program(g, core, T, topo):
+    rank = T.rank_of(core)
+    if rank is None:
+        return
+    do, dma, arrive, ready, finish, wait = make_tracker(g, T)
+
+    def cols(x):
+        if isinstance(x, str):
+            n = T[x].shape[1]
+            return T[x][:, 0:n], (x, 0, n)
+        name, a, b = x[:3]
+        if len(x) == 4:
+            return T[name][:, a:b:x[3]], (name, a, b)
+        return T[name][:, a:b], (name, a, b)
+
+    def ts(out, in0, s1, op0, s2=None, op1=None):
+        o, ro = cols(out)
+        i, ri = cols(in0)
+        rd = [ri]
+        if isinstance(s1, tuple):
+            s1, r1 = cols(s1)
+            rd.append(r1)
+        if isinstance(s2, tuple):
+            s2, r2 = cols(s2)
+            rd.append(r2)
+        if op1 is None:
+            do("v", rd, [ro], lambda e: e.tensor_scalar(o, i, s1, None, op0))
+        else:
+            do("v", rd, [ro], lambda e: e.tensor_scalar(o, i, s1, s2, op0, op1))
+
+    def tt(out, in0, in1, op):
+        o, ro = cols(out)
+        a, ra = cols(in0)
+        b, rb = cols(in1)
+        do("v", [ra, rb], [ro], lambda e: e.tensor_tensor(o, a, b, op))
+
+    def cp(out, in0):
+        o, ro = cols(out)
+        a, ra = cols(in0)
+        do("v", [ra], [ro], lambda e: e.tensor_copy(o, a))
+
+    def gat(out, win, off):
+        o, ro = cols(out)
+        w, rw = cols(win)
+        f, rf = cols(off)
+        do("v", [rw, rf], [ro], lambda e: e.tensor_copy(o, w.indirect(f)))
+
+    def gsub(out, win, off, in1):
+        o, ro = cols(out)
+        w, rw = cols(win)
+        f, rf = cols(off)
+        b, rb = cols(in1)
+        do("v", [rw, rf, rb], [ro], lambda e: e.tensor_tensor(o, w.indirect(f), b, OP.subtract))
+
+    def sca(win, off, in0):
+        w, rw = cols(win)
+        f, rf = cols(off)
+        a, ra = cols(in0)
+        do("v", [rf, ra], [rw], lambda e: e.tensor_copy(w.indirect(f), a))
+
+    def act(out, in0, func, off=None, **kw):
+        o, ro = cols(out)
+        a, ra = cols(in0)
+        rd, wr, kk = [ra], [ro], {}
+        for k, v in kw.items():
+            if isinstance(v, tuple):
+                v, r = cols(v)
+                (wr if k == "accum_out" else rd).append(r)
+            kk[k] = v
+        if off is not None:
+            f, rf = cols(off)
+            a = a.indirect(f)
+            rd.append(rf)
+        do("s", rd, wr, lambda e: e.activation(o, a, func, **kk))
+
+    def mm(out, lhsT, rhs, start, stop):
+        o, ro = cols(out)
+        a, ra = cols(lhsT)
+        b, rb = cols(rhs)
+        do("p", [ra, rb], [ro], lambda e: e.matmul(o, a, b, start, stop))
+
+    def iota(out, pattern, base, cm, flag=True):
+        o, ro = cols(out)
+        if flag:
+            do("g", [], [ro], lambda e: e.iota(o, pattern, base, cm, allow_small_or_imprecise_dtypes=True))
+        else:
+            do("g", [], [ro], lambda e: e.iota(o, pattern, base, cm))
+
+    def sel(buf, op, v):
+        o, ro = cols(buf)
+        do("g", [ro], [ro], lambda e: e.affine_select(o, o, [[1, 128]], op, v, 0, -1))
+
+    def fill(out, v):
+        o, ro = cols(out)
+        do("v", [], [ro], lambda e: e.memset(o, v))
+
+    SW, SD, XW, ZW = ("S", 0, 2048), ("S", 0, 2176), ("ZX", 2048, 4096), ("ZX", 0, 4096)
+
+    dma("s", "ds0", [], ["si"], T.si[:], T.s0[:])
+    dma("y", "dS0", [], [SW], T.S[:, 0:2048], T.stm[:])
+    dma("s", "dw", [], ["wi"], T.wi[:], T.wt[:])
+    dma("y", "dX", [], [XW], T.ZX[:, 2048:4096], T.vx[:])
+    dma("s", "dx0", [], ["xb"], T.xb[:], T.x0[:])
+
+    iota("cp", [[1, 1]], 0, 1, False)
+    iota("cI", [[1, 144]], 0, 0)
+    iota("ex", [[1, 16]], 0, 0)
+    iota("blk", [[16, 8], [0, 16]], 0, 0)
+    iota("tq", [[0, 128]], 1, 0)
+    iota("rc", [[0, 128]], 8192, 0)
+    for name, own in (("tq", 32.0), ("rc", -8192.0)):
+        sel(name, OP.is_gt, 0.0)
+        sel(name, OP.not_equal, own)
+    iota("mk", [[0, 8], [1, 16]], 0, 0)
+    iota("il0", [[16, 8]], 0, 0)
+    iota("l256", [[0, 2], [256, 8]], 0, 0)
+    ts(("cq", 0, 1), "cp", 15, OP.bitwise_and)
+    ts(("cq", 1, 2), "cp", 112, OP.bitwise_and)
+    ts(("cq", 2, 3), "cp", 1, OP.bitwise_and)
+    P, PM, PG, PX, PG16, KM, K0, WC, CTC, XOC = [("cf", j, j + 1) for j in range(10)]
+    cp(P, "cp")
+    cp(("cf", 1, 3), ("cq", 0, 2))
+    ts(PX, ("cq", 2, 3), -2, OP.mult, 1, OP.add)
+    tt(PX, PX, P, OP.add)
+    ts("I16", ("cI", 0, 128), P, OP.is_equal)
+    ts("P16", ("cI", 0, 128), PX, OP.is_equal)
+    ts("rm", "ex", PM, OP.is_equal)
+    for k in range(16):
+        ts(("DA", 128 * k, 128 * k + 128), "I16", ("rm", k, k + 1), OP.mult)
+        ts(("DB", 128 * k, 128 * k + 128), "P16", ("rm", k ^ 1, (k ^ 1) + 1), OP.mult)
+    cp("su", "si")
+    ts("BN", "blk", PG, OP.is_equal, -32.0, OP.mult)
+    ts("I32", "I16", 32.0, OP.mult)
+    ts("sA", "si", -7, OP.add)
+    for m in range(16):
+        ts(("BM", 128 * m, 128 * m + 128), "BN", ("rm", m, m + 1), OP.mult)
+    ts(PG16, PG, 16.0, OP.add)
+    cp(WC, "wi")
+    ts("WT", "cI", PG16, OP.is_equal, WC, OP.mult)
+    ts("BO", "BN", -0.03125, OP.mult)
+    tt("TQ", "tq", "BO", OP.mult)
+    tt("RC", "rc", "BO", OP.mult)
+    ts(KM, PM, -2048.0, OP.add)
+    ts(K0, PM, 0.0, OP.is_equal)
+    ts(CTC, PM, 16.0, OP.mult, 2048.0, OP.add)
+    ts(XOC, PM, 16.0, OP.mult)
+    ts("L1", "cI", PG16, OP.is_equal)
+    ts("LK", "cI", PG16, OP.is_equal, KM, OP.mult)
+
+    def tables():
+        fill(("S", 2048, 2176), 0)
+        fill("on32", 1.0)
+        fill("z16", 0.0)
+        cp("on16", "on32")
+        ts("gm", "il0", PG, OP.is_equal)
+        for q in range(8):
+            ts(("SEL", 128 * q, 128 * q + 128), "on16", ("gm", q, q + 1), OP.mult)
+        cp("GI", "gm")
+        ts("CT", "l256", CTC, OP.add)
+        ts("z16", "z16", P, OP.add)
+        act("z16", "z16", AF.Exp, scale=-math.log(2.0), bias=60.0 * math.log(2.0))
+        ts("THR", "mk", PM, OP.not_equal, 2.0 ** 97, OP.mult)
+        ts("RQ", "gm", 4096.0, OP.mult)
+        ts("IL", "il0", PM, OP.add)
+        ts("XO", ("l256", 0, 8), XOC, OP.add)
+        ts("NIB", "I16", -1.0, OP.mult)
+        ts("IB", "I16", 1.0, OP.mult)
+        ts("BF2", "BN", 32.0, OP.mult)
+        ts("BF1", "BN", 192.0, OP.mult)
+        cp("VJ", "z16")
+        ts(("z16", 0, 1), ("z16", 0, 1), 2.5, OP.mult)
+        ts("THR", "THR", ("z16", 0, 1), OP.max)
+
+    def slm(m):
+        return 16 - m, 144 - m
+
+    def listing(out, tab, rhs, width, last=True):
+        for m in range(16):
+            a, b = slm(m)
+            mm(out, (tab, a, b), (rhs, m, width, 16), m == 0, last and m == 15)
+
+    sent = [0]
+
+    def send(t, src, dst_buf, sem):
+        h = 1 + t % (N - 1)
+        to = T.cores[(rank + h) % N]
+        rid, pid = topo.addr(to)[:2]
+        mask = sum(1 << e for e in topo.engines(core, to)[:NENG])
+        ready("g", [src])
+        g.remote_dma(T[dst_buf][:], T[src][:], T.sem[sem], T.sem.sent, pid, rid, mask)
+        sent[0] += NENG
+        arrive(sem, NENG, [dst_buf])
+
+    c1x, u1, u0 = ("b4", 0, 8), ("b4", 8, 16), ("b4", 16, 24)
+    U = ("b2", 0, 128)
+    FI, SE = ("FS", 0, 128), ("FS", 128, 256)
+    F1, X1, U0 = ("F1X", 0, 128), ("F1X", 128, 256), ("F1X", 256, 384)
+
+    def msg_n(t):
+        listing(("b0", 256, 264), "L1", "F2", 128)
+        ts("mN%d" % t, ("b0", 256, 264), 4097.0, OP.mult, -1.0, OP.add)
+        send(t, "mN%d" % t, "rN%d" % t, "aN%d" % t)
+        if t < RO - 1:
+            act("sg", ("b0", 256, 264), AF.Sign, accum_out=("fc", 0, 1))
+
+    def places():
+        listing(("b1", 256, 272), "LK", "FS", 256, False)
+        mm(("b1", 256, 272), "I16", "CT", False, True)
+
+    def pick():
+        cp("ou", ("b1", 256, 272))
+        act("z2", ZW, AF.Copy, off=("ou", 8, 16))
+        act("z1", ZW, AF.Copy, off=("ou", 0, 8))
+
+    def msg_x(t):
+        mm(("b7", 0, 128), "BF2", SE, True, False)
+        mm(("b7", 0, 128), "IB", "xb", False, False)
+        mm(("b7", 0, 128), "NIB", "z2", False, True)
+        act("mX%d" % t, ("b7", 0, 128), AF.Abs, bias=1024.0)
+        send(t, "mX%d" % t, "rX%d" % t, "aX%d" % t)
+
+    def x_cont():
+        mm(("b7", 128, 256), "BF1", FI, True, False)
+        mm(("b7", 128, 256), "IB", "xb", False, False)
+        mm(("b7", 128, 256), "IB", "z1", False, True)
+
+    def x_base():
+        ts("xv", ("b7", 128, 256), 0.5, OP.mult, 2047.75, OP.add)
+        tt("xba", "xv", "x256", OP.min)
+
+    def merge_x(t):
+        tt("xm", "xba", "rX%d" % t, OP.min)
+        ts("xn", "xm", 255, OP.bitwise_and)
+        cp("xb", "xn")
+
+    def rows():
+        mm(("b7", 256, 264), F1, "GI", True, True)
+        for q in range(8):
+            bk = "b%d" % (5 + q // 4)
+            o = 128 * (q % 4)
+            mm((bk, o, o + 128), ("SEL", 128 * q, 128 * q + 128), F1, True, True)
+
+    def equal():
+        for q in range(8):
+            bk = "b%d" % (5 + q // 4)
+            o = 128 * (q % 4)
+            ts(("EQ", 128 * q, 128 * q + 128), (bk, o, o + 128), ("b7", 256 + q, 257 + q), OP.is_equal)
+
+    def counts():
+        for q in range(8):
+            mm(("b3", 16 * q, 16 * q + 16), ("EQ", 128 * q, 128 * q + 128), "VJ", True, True)
+
+    def rewrite():
+        ts("c1u", c1x, 2048.0, OP.add)
+        cp("c1h", c1x)
+        gat("Sc", SD, "c1u")
+        tt("lt", ("b3", 0, 128), "THR", OP.is_gt)
+        mm(("b3", 256, 264), "lt", "RQ", True, False)
+        mm(("b3", 256, 264), "I16", "c1h", False, True)
+        tt("Sd", "Sc", X1, OP.add)
+
+    def rewrite_end():
+        ts("Sn", "Sd", 2047, OP.bitwise_and)
+        tt("so", ("b3", 256, 264), "IL", OP.min)
+        ts("sou", "so", 2048.0, OP.add)
+        sca(SD, "sou", "Sn")
+
+    def stand():
+        ts("h1", c1x, 0.0, OP.is_lt, 16777216.0, OP.mult)
+        ts("n1", "si", 5, OP.mult)
+        tt("h2", "h1", c1x, OP.add)
+        tt("n2", "n1", u0, OP.add)
+        ts("n3", "n2", 2047, OP.bitwise_and)
+        tt("sb", "h2", "n3", OP.max)
+
+    def variables():
+        cp("x1", u1)
+        ts("x2", "x1", 15, OP.bitwise_and)
+        tt("x3", "x2", "XO", OP.add)
+        cp("xou", "x3")
+        sca(XW, "xou", "z1")
+
+    def alist(q):
+        a = 128 * (q // 2) + CH * (q % 2)
+        return ("ABT", a, a + CH)
+
+    def blist(q):
+        a = 128 * (q // 2) + 64 + CH * (q % 2)
+        return ("ABT", a, a + CH)
+
+    def xbg(q):
+        act(("XB", 512 * q, 512 * q + 512), XW, AF.Copy, off=blist(q))
+
+    def xag(q):
+        gsub(("DD", 512 * q, 512 * q + 512), XW, alist(q), ("XB", 512 * q, 512 * q + 512))
+
+    def zab(q):
+        act(("ZX", 512 * q, 512 * q + 512), ("DD", 512 * q, 512 * q + 512), AF.Abs)
+
+    for t in range(RO):
+        last = t == RO - 1
+        gat("Cu", SW, "su")
+        gat("G0", SW, ("Cu", 0, 64))
+        if t:
+            ts("sA", "si", ("b2", 256, 257), OP.subtract, 7.0, OP.subtract)
+        ts("C16", "Cu", 1, OP.add)
+        gat("G1", SW, ("Cu", 64, 128))
+        for h in range(2):
+            for tab, o in (("DA", 0), ("DB", 64)):
+                for k in range(16):
+                    mm(("b%d" % h, o, o + 64), (tab, 128 * k, 128 * k + 128), ("G%d" % h, k, 1024, 16), k == 0, k == 15)
+        mm(("b3", 256, 384), "I16", "C16", True, True)
+        for m in range(16):
+            o = ("b2", 128 + m, 256, 16)
+            mm(o, ("BM", 128 * m, 128 * m + 128), "sA", True, False)
+            mm(o, "I32", ("C16", m, 128, 16), False, True)
+        cp(("ABT", 0, 128), ("b0", 0, 128))
+        gat(("XB", 0, 512), XW, blist(0))
+        xbg(1)
+        cp(("ABT", 128, 256), ("b1", 0, 128))
+        xag(0)
+        xbg(2)
+        zab(0)
+        xag(1)
+        xbg(3)
+        zab(1)
+        xag(2)
+        zab(2)
+        xag(3)
+        zab(3)
+        if t == 0:
+            act("x256", "xb", AF.Identity, bias=256.0)
+        for h in range(2):
+            for k in range(16):
+                a, b = slm(k)
+                mm(("b2", 64 * h, 64 * h + 64), ("WT", a, b), ("ZX", 1024 * h + k, 1024 * h + 1024, 16), k == 0, k == 15)
+        if t:
+            x_base()
+            merge_x(t - 1)
+            act("x256", "xb", AF.Identity, bias=256.0)
+        else:
+            tables()
+        ts("ui", U, 16, OP.add)
+        ts("w2", "ui", 255, OP.bitwise_and)
+        tt("sq", "w2", "w2", OP.mult)
+        tt("y", "sq", ("b2", 128, 256), OP.add)
+        ts("yy", "y", 480, OP.bitwise_and)
+        ts("cl", "yy", 0, OP.is_equal)
+        mm(("b3", 0, 128), "TQ", "cl", True, True)
+        mm(("b3", 128, 256), "RC", "cl", True, False)
+        mm(("b3", 128, 256), "I16", "C16", False, True)
+        ts("uk", "ui", 2047, OP.bitwise_and)
+        ts("ukf", "uk", -16, OP.add)
+        ts(U0, "ukf", K0, OP.mult)
+        ts(SE, ("b3", 0, 128), 33.0, OP.is_equal)
+        if not last:
+            tt("F2", SE, ("b3", 256, 384), OP.mult)
+            ts(F1, ("b3", 128, 256), 6143.0, OP.add, 0.0, OP.min)
+            ts(FI, ("b3", 0, 128), 32.0, OP.is_equal)
+            tt(X1, FI, "ukf", OP.mult)
+            msg_n(t)
+            rows()
+            listing(("b4", 0, 24), "L1", "F1X", 384)
+            equal()
+            counts()
+            places()
+            rewrite()
+            pick()
+            mm(("b2", 256, 257), "on32", "fc", True, True)
+            msg_x(t)
+            x_cont()
+            rewrite_end()
+            stand()
+            variables()
+        else:
+            ts(FI, ("b3", 0, 128), 32.0, OP.is_equal)
+            places()
+            tt("F2", SE, ("b3", 256, 384), OP.mult)
+            ts(F1, ("b3", 128, 256), 6143.0, OP.add, 0.0, OP.min)
+            tt(X1, FI, "ukf", OP.mult)
+            pick()
+            listing(("b4", 0, 24), "L1", "F1X", 384)
+            msg_x(t)
+            msg_n(t)
+            rows()
+            variables()
+            dma("y", "oV", [XW], [], T.yv[:], T.ZX[:, 2048:4096])
+            equal()
+            counts()
+            x_cont()
+            rewrite()
+            rewrite_end()
+            stand()
+            x_base()
+            acc = ("b5", 0, 256)
+            tt(acc, ("S", 0, 256), ("S", 256, 512), OP.add)
+            for q in range(2, 6):
+                tt(acc, acc, ("S", 256 * q, 256 * q + 256), OP.add)
+        tt("se", "sb", "rN%d" % t, OP.max)
+        ts("si", "se", 2047, OP.bitwise_and)
+        if not last:
+            cp("su", "si")
+    cp("sf", "si")
+    merge_x(RO - 1)
+    dma("y", "oX", ["xb"], [], T.yx[:], T.xb[:])
+    dma("s", "oS", ["sf"], [], T.ys[:], T.sf[:])
+    tt(acc, acc, ("S", 1536, 1792), OP.add)
+    tt("yto", acc, ("S", 1792, 2048), OP.add)
+    dma("s", "oT", ["yto"], [], T.yt[:], T.yto[:])
+    g.wait_ge(T.sem.sent, sent[0])
+    for s in ("ds0", "dS0", "dw", "dX", "dx0", "oV", "oT", "oS", "oX"):
+        wait("g", {s: 16})
+    finish()

@@ -4,6 +4,8 @@ from concourse.mybir import AluOpType as OP, ActivationFunctionType as AF
 N, RO = 8, 3
 NENG = 8
 CH = 32
+VB = (0,)
+SQ = 4
 
 F32, F16, BF, I4, U2 = "float32", "float16", "bfloat16", "int32", "uint16"
 SCRATCH = {}
@@ -18,16 +20,16 @@ _sb(I4, S=2176, si=8, wi=1)
 _sb(BF, ZX=4096, xb=128)
 _sb(U2, su=8)
 _sb(I4, cp=1, cq=4)
-_sb(F32, cI=144, cf=16, tq=128, rc=128, blk=128, mk=128, l256=16, rm=16, gm=8, ex=16, z16=16, THR=128, IL=8, XO=8, on32=128, il0=8)
-_sb(F16, I16=128, P16=128, I32=128, L1=144, LK=144, DA=2048, DB=2048, BM=2048, BN=128, SEL=1024, on16=128, TQ=128, RC=128,
+_sb(F32, cI=144, cf=16, tq=128, rc=128, blk=128, mk=128, l256=16, rm=16, gm=8, ex=16, z16=16, THR=128, IL=8, XO=8, il0=8, pf=16)
+_sb(F16, I16=128, P16=128, I32=128, L1=144, LK=144, DA=2048, DB=2048, BN=128, SEL=1024, on16=128, TQ=128, RC=128,
     BO=128, BF1=128, BF2=128, RQ=8, GI=8, CT=16)
-_sb(BF, IB=128, NIB=128, WT=144, VJ=16)
+_sb(BF, TB=2048, SL=128, FCB=128, ONB=128, IB=128, NIB=128, WT=144, VJ=16)
 _sb(U2, Cu=128, ABT=256, ou=16, c1u=8, sou=8, xou=8)
-_sb(F16, C16=128, G0=1024, G1=1024, sA=8, cl=128, ukf=128, FS=256, F1X=384, F2=128, lt=128, c1h=8)
-_sb(BF, XB=2048, DD=2048, EQ=1024, z1=128, z2=128, sg=8)
+_sb(F16, C16=128, G0=1024, G1=1024, cl=128, ukf=128, FS=256, F1X=384, F2=128, lt=128, c1h=8)
+_sb(BF, XB=2048, DD=2048, EQ=1024, EN=1024, z1=128, z2=128, sg=8)
 _sb(I4, ui=128, w2=128, sq=128, y=128, yy=128, uk=128, Sc=128, Sd=128, Sn=128, x1=8, x2=8, x3=8, n2=8, n3=8, se=8, xv=128,
-    xba=128, xm=128, xn=128)
-_sb(F32, so=8, n1=8, h1=8, h2=8, sb=8, fc=1, x256=128, sf=8, yto=256)
+    xm=128, xn=128)
+_sb(F32, col=8, cola=8, so=8, n1=8, h1=8, h2=8, sb=8, fc=1, sf=8, yto=256)
 SEMAPHORES = ["qv", "qs", "qp", "qg", "dS0", "dX", "dx0", "dw", "ds0", "oV", "oT", "oX", "oS", "sent"]
 for _t in range(RO):
     _sb(F32, **{"mN%d" % _t: 8, "rN%d" % _t: 8})
@@ -37,91 +39,147 @@ PSUM = ["b%d" % _b for _b in range(8)]
 for _b in PSUM:
     SCRATCH[_b] = ("psum", [128, 512], F32)
 
+CYC, PECYC, GATH, SCAT, WAKE, LOCAL, FLIGHT = 0.0012, 0.0005, 2.0, 3.8, 0.06, 2.0, 3.0
 
-def make_tracker(g, T):
+
+def make_plan(g, T):
     eng = {"v": g.vector, "s": g.scalar, "p": g.tensor, "g": g, "y": g.sync}
-    sem = {"v": "qv", "s": "qs", "p": "qp", "g": "qg"}
-    count = {}
-    clock = dict((q, {}) for q in eng)
-    event = {}
+    qsem = {"v": "qv", "s": "qs", "p": "qp", "g": "qg"}
+    nodes = []
     hist = {}
-
-    def deps(q, rd, wr):
-        need = {}
-        for acc, isw in ((rd, False), (wr, True)):
-            for name, a, b in acc:
-                for (a0, b0, w0, src, n) in hist.get(name, []):
-                    if name in PSUM:
-                        hit = (src != q) or (q != "p" and a < b0 and a0 < b and (isw or w0))
-                    else:
-                        hit = a < b0 and a0 < b and (isw or w0)
-                    if hit and n > clock[q].get(src, 0):
-                        need[src] = max(need.get(src, 0), n)
-        return need
-
-    def wait(q, need):
-        for src in sorted(need):
-            n = need[src]
-            if any(event[(o, need[o])].get(src, 0) >= n for o in need if o != src):
-                continue
-            eng[q].wait_ge(T.sem[sem.get(src, src)], n)
-        for src in need:
-            for k, m in event[(src, need[src])].items():
-                clock[q][k] = max(clock[q].get(k, 0), m)
-
-    def note(src, n, q, rd, wr):
-        ev = dict(clock[q])
-        ev[src] = n
-        event[(src, n)] = ev
-        for name, a, b in wr:
-            keep = []
-            for h in hist.get(name, []):
-                if not (a <= h[0] and h[1] <= b and ev.get(h[3], 0) >= h[4]):
-                    keep.append(h)
-            hist[name] = keep + [(a, b, True, src, n)]
-        for name, a, b in rd:
-            keep = [h for h in hist.get(name, []) if h[2] or h[3] != src or not (a <= h[0] and h[1] <= b)]
-            hist[name] = keep + [(a, b, False, src, n)]
 
     def rng(x):
         return (x, 0, T[x].shape[1]) if isinstance(x, str) else x
 
-    def do(q, rd, wr, fn):
+    def add(q, rd, wr, fns, dur, sem=None, inc=1, lat=0.0, after=None):
+        i = len(nodes)
         rd = [rng(x) for x in rd]
         wr = [rng(x) for x in wr]
-        wait(q, deps(q, rd, wr))
-        n = count.get(q, 0) + 1
-        count[q] = n
-        fn(eng[q]).then_inc(T.sem[sem[q]], 1)
-        note(q, n, q, rd, wr)
+        pred = {}
+        for acc, isw in ((rd, False), (wr, True)):
+            for name, a, b in acc:
+                for (a0, b0, w0, j) in hist.get(name, []):
+                    over = a < b0 and a0 < b and (isw or w0)
+                    if name in PSUM:
+                        if nodes[j]["q"] != q or (over and q != "p"):
+                            pred[j] = True
+                        elif over:
+                            pred.setdefault(j, False)
+                    elif over:
+                        pred[j] = True
+        if after is not None:
+            pred[after] = False
+        nodes.append({"q": q, "fns": fns, "dur": dur, "sem": sem, "inc": inc, "lat": lat, "pred": pred, "i": i})
+        for name, a, b in wr:
+            keep = [h for h in hist.get(name, []) if not (a <= h[0] and h[1] <= b and h[3] in pred)]
+            hist[name] = keep + [(a, b, True, i)]
+        for name, a, b in rd:
+            hist[name] = hist.get(name, []) + [(a, b, False, i)]
+        return i
 
-    def dma(q, s, rd, wr, out, in_):
-        rd = [rng(x) for x in rd]
-        wr = [rng(x) for x in wr]
-        wait(q, deps(q, rd, wr))
-        eng[q].dma_start(out, in_).then_inc(T.sem[s], 16)
-        note(s, 16, q, rd, wr)
+    def order():
+        n = len(nodes)
+        succ = [[] for _ in nodes]
+        for x in nodes:
+            for j, w in x["pred"].items():
+                succ[j].append((x["i"], w))
+        prio = [0.0] * n
+        for i in range(n - 1, -1, -1):
+            x = nodes[i]
+            best = max([prio[j] + (WAKE if w else 0.0) for j, w in succ[i]] + [0.0])
+            prio[i] = best + x["dur"] + x["lat"]
+        left = [len(x["pred"]) for x in nodes]
+        ready = [0.0] * n
+        free = {}
+        avail = {}
+        for x in nodes:
+            if not left[x["i"]]:
+                avail.setdefault(x["q"], []).append(x["i"])
+        out = []
+        while any(avail.values()):
+            pick = None
+            for q in avail:
+                if not avail[q]:
+                    continue
+                fr = free.get(q, 0.0) if q != "n" else 0.0
+                t0 = min(max(fr, ready[i]) for i in avail[q])
+                c = [i for i in avail[q] if max(fr, ready[i]) <= t0 + 0.02]
+                i = max(c, key=lambda k: prio[k])
+                t1 = max(fr, ready[i])
+                if pick is None or t1 < pick[0]:
+                    pick = (t1, i, q)
+            t1, i, q = pick
+            avail[q].remove(i)
+            x = nodes[i]
+            end = t1 + x["dur"]
+            free[q] = end
+            out.append(i)
+            for j, w in succ[i]:
+                ready[j] = max(ready[j], end + x["lat"] + (WAKE if w else 0.0))
+                left[j] -= 1
+                if not left[j]:
+                    avail.setdefault(nodes[j]["q"], []).append(j)
+        return out
 
-    def arrive(s, n, wr):
-        event[(s, n)] = {s: n}
-        for x in wr:
-            hist[x] = [rng(x)[1:] + (True, s, n)]
+    def emit():
+        count = {}
+        clock = dict((q, {}) for q in eng)
+        event = {}
+        where = {}
 
-    def ready(q, rd):
-        wait(q, deps(q, [rng(x) for x in rd], []))
+        def wait(q, need):
+            for src in sorted(need):
+                if not any(event[(o, need[o])].get(src, 0) >= need[src] for o in need if o != src):
+                    eng[q].wait_ge(T.sem[qsem.get(src, src)], need[src])
+            for src in need:
+                for k, m in event[(src, need[src])].items():
+                    clock[q][k] = max(clock[q].get(k, 0), m)
 
-    def finish():
+        seq = order()
+        for i in seq:
+            x = nodes[i]
+            q = x["q"]
+            if q == "n":
+                where[i] = (x["sem"], x["inc"])
+                event[where[i]] = {x["sem"]: x["inc"]}
+                continue
+            need = {}
+            for j, w in x["pred"].items():
+                if w:
+                    src, n = where[j]
+                    if n > clock[q].get(src, 0):
+                        need[src] = max(need.get(src, 0), n)
+            wait(q, need)
+            if x["sem"] is None:
+                for fn in x["fns"]:
+                    fn(eng[q]).then_inc(T.sem[qsem[q]], 1)
+                    count[q] = count.get(q, 0) + 1
+                where[i] = (q, count[q])
+            else:
+                for fn in x["fns"]:
+                    ins = fn(eng[q])
+                    if x["sem"] != "sent":
+                        ins.then_inc(T.sem[x["sem"]], 16)
+                where[i] = (x["sem"], x["inc"])
+            ev = dict(clock[q])
+            ev[where[i][0]] = where[i][1]
+            event[where[i]] = ev
+        for x in nodes:
+            if x["sem"] is not None and x["sem"] != "sent" and x["q"] != "n" and x["inc"] > clock["g"].get(x["sem"], 0):
+                wait("g", {x["sem"]: x["inc"]})
+        g.wait_ge(T.sem.sent, sum(x["inc"] for x in nodes if x["sem"] == "sent"))
         for q in ("v", "s", "p", "g"):
-            if count.get(q, 0) > clock["g"].get(q, 0):
+            if count[q] > clock["g"].get(q, 0):
                 wait("g", {q: count[q]})
-    return do, dma, arrive, ready, finish, wait
+        return nodes, seq
+    return add, emit
 
 
 def rank_program(g, core, T, topo):
     rank = T.rank_of(core)
     if rank is None:
         return
-    do, dma, arrive, ready, finish, wait = make_tracker(g, T)
+    add, emit = make_plan(g, T)
 
     def cols(x):
         if isinstance(x, str):
@@ -132,55 +190,58 @@ def rank_program(g, core, T, topo):
             return T[name][:, a:b:x[3]], (name, a, b)
         return T[name][:, a:b], (name, a, b)
 
+    def width(x):
+        r = cols(x)[1]
+        return (r[2] - r[1]) // (x[3] if len(x) == 4 and not isinstance(x, str) else 1)
+
+    def buf(x):
+        return x if isinstance(x, str) else x[0]
+
+    def small(*xs):
+        return all(SCRATCH[buf(x)][2] in (F16, BF, U2) for x in xs)
+
+    def vec(ins, out, fn, cyc):
+        add("v", [cols(x)[1] for x in ins], [cols(out)[1]], [fn], CYC * max(64, cyc))
+
     def ts(out, in0, s1, op0, s2=None, op1=None):
-        o, ro = cols(out)
-        i, ri = cols(in0)
-        rd = [ri]
-        if isinstance(s1, tuple):
-            s1, r1 = cols(s1)
-            rd.append(r1)
-        if isinstance(s2, tuple):
-            s2, r2 = cols(s2)
-            rd.append(r2)
+        o, i = cols(out)[0], cols(in0)[0]
+        rd = [in0] + [x for x in (s1, s2) if isinstance(x, tuple)]
+        s1 = cols(s1)[0] if isinstance(s1, tuple) else s1
+        s2 = cols(s2)[0] if isinstance(s2, tuple) else s2
         if op1 is None:
-            do("v", rd, [ro], lambda e: e.tensor_scalar(o, i, s1, None, op0))
+            fn = lambda e: e.tensor_scalar(o, i, s1, None, op0)
         else:
-            do("v", rd, [ro], lambda e: e.tensor_scalar(o, i, s1, s2, op0, op1))
+            fn = lambda e: e.tensor_scalar(o, i, s1, s2, op0, op1)
+        vec(rd, out, fn, width(out) * (0.5 if small(out, in0) else 1))
 
     def tt(out, in0, in1, op):
-        o, ro = cols(out)
-        a, ra = cols(in0)
-        b, rb = cols(in1)
-        do("v", [ra, rb], [ro], lambda e: e.tensor_tensor(o, a, b, op))
+        o, a, b = cols(out)[0], cols(in0)[0], cols(in1)[0]
+        ps = buf(in0) in PSUM or buf(in1) in PSUM
+        vec([in0, in1], out, lambda e: e.tensor_tensor(o, a, b, op), width(out) * (1 if ps else 2))
 
     def cp(out, in0):
-        o, ro = cols(out)
-        a, ra = cols(in0)
-        do("v", [ra], [ro], lambda e: e.tensor_copy(o, a))
+        o, a = cols(out)[0], cols(in0)[0]
+        vec([in0], out, lambda e: e.tensor_copy(o, a), width(out) * (0.5 if small(out, in0) else 1))
 
     def gat(out, win, off):
-        o, ro = cols(out)
-        w, rw = cols(win)
-        f, rf = cols(off)
-        do("v", [rw, rf], [ro], lambda e: e.tensor_copy(o, w.indirect(f)))
+        o, w, f = cols(out)[0], cols(win)[0], cols(off)[0]
+        vec([win, off], out, lambda e: e.tensor_copy(o, w.indirect(f)), 50 + GATH * width(out))
 
     def gsub(out, win, off, in1):
-        o, ro = cols(out)
-        w, rw = cols(win)
-        f, rf = cols(off)
-        b, rb = cols(in1)
-        do("v", [rw, rf, rb], [ro], lambda e: e.tensor_tensor(o, w.indirect(f), b, OP.subtract))
+        o, w, f, b = cols(out)[0], cols(win)[0], cols(off)[0], cols(in1)[0]
+        vec([win, off, in1], out, lambda e: e.tensor_tensor(o, w.indirect(f), b, OP.subtract), 50 + GATH * width(out))
 
     def sca(win, off, in0):
-        w, rw = cols(win)
-        f, rf = cols(off)
-        a, ra = cols(in0)
-        do("v", [rf, ra], [rw], lambda e: e.tensor_copy(w.indirect(f), a))
+        w, f, a = cols(win)[0], cols(off)[0], cols(in0)[0]
+        vec([off, in0], win, lambda e: e.tensor_copy(w.indirect(f), a), 50 + SCAT * width(in0))
+
+    def fill(out, v):
+        o = cols(out)[0]
+        vec([], out, lambda e: e.memset(o, v), width(out))
 
     def act(out, in0, func, off=None, **kw):
-        o, ro = cols(out)
-        a, ra = cols(in0)
-        rd, wr, kk = [ra], [ro], {}
+        o, a = cols(out)[0], cols(in0)[0]
+        rd, wr, kk = [cols(in0)[1]], [cols(out)[1]], {}
         for k, v in kw.items():
             if isinstance(v, tuple):
                 v, r = cols(v)
@@ -190,38 +251,42 @@ def rank_program(g, core, T, topo):
             f, rf = cols(off)
             a = a.indirect(f)
             rd.append(rf)
-        do("s", rd, wr, lambda e: e.activation(o, a, func, **kk))
+        add("s", rd, wr, [lambda e: e.activation(o, a, func, **kk)], CYC * (65 + width(out) * (GATH if off is not None else 1)))
 
-    def mm(out, lhsT, rhs, start, stop):
-        o, ro = cols(out)
-        a, ra = cols(lhsT)
-        b, rb = cols(rhs)
-        do("p", [ra, rb], [ro], lambda e: e.matmul(o, a, b, start, stop))
+    def one(x):
+        o, a, b = cols(x[0])[0], cols(x[1])[0], cols(x[2])[0]
+        return lambda e: e.matmul(o, a, b, x[3], x[4])
+
+    def mms(xs):
+        rd = sorted(set(cols(x[1])[1] for x in xs) | set(cols(x[2])[1] for x in xs))
+        wr = sorted(set(cols(x[0])[1] for x in xs))
+        add("p", rd, wr, [one(x) for x in xs], sum(max(64, width(x[0])) * PECYC for x in xs))
 
     def iota(out, pattern, base, cm, flag=True):
-        o, ro = cols(out)
+        o = cols(out)[0]
         if flag:
-            do("g", [], [ro], lambda e: e.iota(o, pattern, base, cm, allow_small_or_imprecise_dtypes=True))
+            fn = lambda e: e.iota(o, pattern, base, cm, allow_small_or_imprecise_dtypes=True)
         else:
-            do("g", [], [ro], lambda e: e.iota(o, pattern, base, cm))
+            fn = lambda e: e.iota(o, pattern, base, cm)
+        add("g", [], [cols(out)[1]], [fn], 0.13 + 2 * CYC * width(out))
 
-    def sel(buf, op, v):
-        o, ro = cols(buf)
-        do("g", [ro], [ro], lambda e: e.affine_select(o, o, [[1, 128]], op, v, 0, -1))
-
-    def fill(out, v):
+    def sel(out, op, v):
         o, ro = cols(out)
-        do("v", [], [ro], lambda e: e.memset(o, v))
+        add("g", [ro], [ro], [lambda e: e.affine_select(o, o, [[1, 128]], op, v, 0, -1)], 0.17 + 2 * CYC * width(out))
+
+    def dma(q, s, rd, wr, out, in_, us):
+        add(q, rd, wr, [lambda e: e.dma_start(out, in_)], 0.1, sem=s, inc=16, lat=us)
 
     SW, SD, XW, ZW = ("S", 0, 2048), ("S", 0, 2176), ("ZX", 2048, 4096), ("ZX", 0, 4096)
 
-    dma("s", "ds0", [], ["si"], T.si[:], T.s0[:])
-    dma("y", "dS0", [], [SW], T.S[:, 0:2048], T.stm[:])
-    dma("s", "dw", [], ["wi"], T.wi[:], T.wt[:])
-    dma("y", "dX", [], [XW], T.ZX[:, 2048:4096], T.vx[:])
-    dma("s", "dx0", [], ["xb"], T.xb[:], T.x0[:])
+    dma("s", "ds0", [], ["si"], T.si[:], T.s0[:], LOCAL)
+    dma("y", "dS0", [], [SW], T.S[:, 0:2048], T.stm[:], 6.0)
+    dma("s", "dw", [], ["wi"], T.wi[:], T.wt[:], LOCAL)
+    dma("y", "dX", [], [XW], T.ZX[:, 2048:4096], T.vx[:], 9.0)
+    dma("s", "dx0", [], ["xb"], T.xb[:], T.x0[:], LOCAL)
 
     iota("cp", [[1, 1]], 0, 1, False)
+    iota("pf", [[0, 16]], 0, 1)
     iota("cI", [[1, 144]], 0, 0)
     iota("ex", [[1, 16]], 0, 0)
     iota("blk", [[16, 8], [0, 16]], 0, 0)
@@ -230,14 +295,15 @@ def rank_program(g, core, T, topo):
     for name, own in (("tq", 32.0), ("rc", -8192.0)):
         sel(name, OP.is_gt, 0.0)
         sel(name, OP.not_equal, own)
+    iota("TB", [[0, 128], [-32, 16]], 224, 0)
     iota("mk", [[0, 8], [1, 16]], 0, 0)
     iota("il0", [[16, 8]], 0, 0)
     iota("l256", [[0, 2], [256, 8]], 0, 0)
+    P = ("pf", 0, 1)
+    PX, PM, PG, PG16, KM, K0, WC, CTC, XOC = [("cf", j, j + 1) for j in range(9)]
     ts(("cq", 0, 1), "cp", 15, OP.bitwise_and)
     ts(("cq", 1, 2), "cp", 112, OP.bitwise_and)
     ts(("cq", 2, 3), "cp", 1, OP.bitwise_and)
-    P, PM, PG, PX, PG16, KM, K0, WC, CTC, XOC = [("cf", j, j + 1) for j in range(10)]
-    cp(P, "cp")
     cp(("cf", 1, 3), ("cq", 0, 2))
     ts(PX, ("cq", 2, 3), -2, OP.mult, 1, OP.add)
     tt(PX, PX, P, OP.add)
@@ -250,9 +316,8 @@ def rank_program(g, core, T, topo):
     cp("su", "si")
     ts("BN", "blk", PG, OP.is_equal, -32.0, OP.mult)
     ts("I32", "I16", 32.0, OP.mult)
-    ts("sA", "si", -7, OP.add)
-    for m in range(16):
-        ts(("BM", 128 * m, 128 * m + 128), "BN", ("rm", m, m + 1), OP.mult)
+    ts("IB", "I16", 1.0, OP.mult)
+    fill("ONB", 32.0)
     ts(PG16, PG, 16.0, OP.add)
     cp(WC, "wi")
     ts("WT", "cI", PG16, OP.is_equal, WC, OP.mult)
@@ -265,139 +330,46 @@ def rank_program(g, core, T, topo):
     ts(XOC, PM, 16.0, OP.mult)
     ts("L1", "cI", PG16, OP.is_equal)
     ts("LK", "cI", PG16, OP.is_equal, KM, OP.mult)
-
-    def tables():
-        fill(("S", 2048, 2176), 0)
-        fill("on32", 1.0)
-        fill("z16", 0.0)
-        cp("on16", "on32")
-        ts("gm", "il0", PG, OP.is_equal)
-        for q in range(8):
-            ts(("SEL", 128 * q, 128 * q + 128), "on16", ("gm", q, q + 1), OP.mult)
-        cp("GI", "gm")
-        ts("CT", "l256", CTC, OP.add)
-        ts("z16", "z16", P, OP.add)
-        act("z16", "z16", AF.Exp, scale=-math.log(2.0), bias=60.0 * math.log(2.0))
-        ts("THR", "mk", PM, OP.not_equal, 2.0 ** 97, OP.mult)
-        ts("RQ", "gm", 4096.0, OP.mult)
-        ts("IL", "il0", PM, OP.add)
-        ts("XO", ("l256", 0, 8), XOC, OP.add)
-        ts("NIB", "I16", -1.0, OP.mult)
-        ts("IB", "I16", 1.0, OP.mult)
-        ts("BF2", "BN", 32.0, OP.mult)
-        ts("BF1", "BN", 192.0, OP.mult)
-        cp("VJ", "z16")
-        ts(("z16", 0, 1), ("z16", 0, 1), 2.5, OP.mult)
-        ts("THR", "THR", ("z16", 0, 1), OP.max)
+    fill(("S", 2048, 2176), 0)
+    ts("on16", ("cI", 0, 128), 0.0, OP.mult, 1.0, OP.add)
+    ts("gm", "il0", PG, OP.is_equal)
+    for q in range(8):
+        ts(("SEL", 128 * q, 128 * q + 128), "on16", ("gm", q, q + 1), OP.mult)
+    cp("GI", "gm")
+    ts("CT", "l256", CTC, OP.add)
+    act("z16", "pf", AF.Exp, scale=-math.log(2.0), bias=60.0 * math.log(2.0))
+    ts("THR", "mk", PM, OP.not_equal, 2.0 ** 97, OP.mult)
+    ts("RQ", "gm", 4096.0, OP.mult)
+    ts("IL", "il0", PM, OP.add)
+    ts("XO", ("l256", 0, 8), XOC, OP.add)
+    ts("NIB", "I16", -1.0, OP.mult)
+    ts("BF2", "BN", 32.0, OP.mult)
+    ts("BF1", "BN", 192.0, OP.mult)
+    cp("VJ", "z16")
+    ts(("z16", 0, 1), ("z16", 0, 1), 2.5, OP.mult)
+    ts("THR", "THR", ("z16", 0, 1), OP.max)
 
     def slm(m):
         return 16 - m, 144 - m
 
-    def listing(out, tab, rhs, width, last=True):
-        for m in range(16):
-            a, b = slm(m)
-            mm(out, (tab, a, b), (rhs, m, width, 16), m == 0, last and m == 15)
-
-    sent = [0]
+    def listing(out, tab, rhs, wid, more=None):
+        xs = [(out, (tab,) + slm(m), (rhs, m, wid, 16), m == 0, more is None and m == 15) for m in range(16)]
+        if more is not None:
+            xs.append((out, more[0], more[1], False, True))
+        mms(xs)
 
     def send(t, src, dst_buf, sem):
-        h = 1 + t % (N - 1)
-        to = T.cores[(rank + h) % N]
+        to = T.cores[(rank + 1 + t % (N - 1)) % N]
         rid, pid = topo.addr(to)[:2]
         mask = sum(1 << e for e in topo.engines(core, to)[:NENG])
-        ready("g", [src])
-        g.remote_dma(T[dst_buf][:], T[src][:], T.sem[sem], T.sem.sent, pid, rid, mask)
-        sent[0] += NENG
-        arrive(sem, NENG, [dst_buf])
+        i = add("g", [src], [], [lambda e: e.remote_dma(T[dst_buf][:], T[src][:], T.sem[sem], T.sem.sent, pid, rid, mask)], 0.3,
+                sem="sent", inc=NENG)
+        add("n", [], [dst_buf], [], 0.0, sem=sem, inc=NENG, lat=FLIGHT, after=i)
 
-    c1x, u1, u0 = ("b4", 0, 8), ("b4", 8, 16), ("b4", 16, 24)
-    U = ("b2", 0, 128)
-    FI, SE = ("FS", 0, 128), ("FS", 128, 256)
-    F1, X1, U0 = ("F1X", 0, 128), ("F1X", 128, 256), ("F1X", 256, 384)
-
-    def msg_n(t):
-        listing(("b0", 256, 264), "L1", "F2", 128)
-        ts("mN%d" % t, ("b0", 256, 264), 4097.0, OP.mult, -1.0, OP.add)
-        send(t, "mN%d" % t, "rN%d" % t, "aN%d" % t)
-        if t < RO - 1:
-            act("sg", ("b0", 256, 264), AF.Sign, accum_out=("fc", 0, 1))
-
-    def places():
-        listing(("b1", 256, 272), "LK", "FS", 256, False)
-        mm(("b1", 256, 272), "I16", "CT", False, True)
-
-    def pick():
-        cp("ou", ("b1", 256, 272))
-        act("z2", ZW, AF.Copy, off=("ou", 8, 16))
-        act("z1", ZW, AF.Copy, off=("ou", 0, 8))
-
-    def msg_x(t):
-        mm(("b7", 0, 128), "BF2", SE, True, False)
-        mm(("b7", 0, 128), "IB", "xb", False, False)
-        mm(("b7", 0, 128), "NIB", "z2", False, True)
-        act("mX%d" % t, ("b7", 0, 128), AF.Abs, bias=1024.0)
-        send(t, "mX%d" % t, "rX%d" % t, "aX%d" % t)
-
-    def x_cont():
-        mm(("b7", 128, 256), "BF1", FI, True, False)
-        mm(("b7", 128, 256), "IB", "xb", False, False)
-        mm(("b7", 128, 256), "IB", "z1", False, True)
-
-    def x_base():
-        ts("xv", ("b7", 128, 256), 0.5, OP.mult, 2047.75, OP.add)
-        tt("xba", "xv", "x256", OP.min)
-
-    def merge_x(t):
-        tt("xm", "xba", "rX%d" % t, OP.min)
-        ts("xn", "xm", 255, OP.bitwise_and)
-        cp("xb", "xn")
-
-    def rows():
-        mm(("b7", 256, 264), F1, "GI", True, True)
-        for q in range(8):
-            bk = "b%d" % (5 + q // 4)
-            o = 128 * (q % 4)
-            mm((bk, o, o + 128), ("SEL", 128 * q, 128 * q + 128), F1, True, True)
-
-    def equal():
-        for q in range(8):
-            bk = "b%d" % (5 + q // 4)
-            o = 128 * (q % 4)
-            ts(("EQ", 128 * q, 128 * q + 128), (bk, o, o + 128), ("b7", 256 + q, 257 + q), OP.is_equal)
-
-    def counts():
-        for q in range(8):
-            mm(("b3", 16 * q, 16 * q + 16), ("EQ", 128 * q, 128 * q + 128), "VJ", True, True)
-
-    def rewrite():
-        ts("c1u", c1x, 2048.0, OP.add)
-        cp("c1h", c1x)
-        gat("Sc", SD, "c1u")
-        tt("lt", ("b3", 0, 128), "THR", OP.is_gt)
-        mm(("b3", 256, 264), "lt", "RQ", True, False)
-        mm(("b3", 256, 264), "I16", "c1h", False, True)
-        tt("Sd", "Sc", X1, OP.add)
-
-    def rewrite_end():
-        ts("Sn", "Sd", 2047, OP.bitwise_and)
-        tt("so", ("b3", 256, 264), "IL", OP.min)
-        ts("sou", "so", 2048.0, OP.add)
-        sca(SD, "sou", "Sn")
-
-    def stand():
-        ts("h1", c1x, 0.0, OP.is_lt, 16777216.0, OP.mult)
-        ts("n1", "si", 5, OP.mult)
-        tt("h2", "h1", c1x, OP.add)
-        tt("n2", "n1", u0, OP.add)
-        ts("n3", "n2", 2047, OP.bitwise_and)
-        tt("sb", "h2", "n3", OP.max)
-
-    def variables():
-        cp("x1", u1)
-        ts("x2", "x1", 15, OP.bitwise_and)
-        tt("x3", "x2", "XO", OP.add)
-        cp("xou", "x3")
-        sca(XW, "xou", "z1")
+    def hf(x, h):
+        if isinstance(x, str):
+            x = (x, 0, 128)
+        return (x[0], x[1] + 64 * h, x[1] + 64 * h + 64)
 
     def alist(q):
         a = 128 * (q // 2) + CH * (q % 2)
@@ -407,126 +379,133 @@ def rank_program(g, core, T, topo):
         a = 128 * (q // 2) + 64 + CH * (q % 2)
         return ("ABT", a, a + CH)
 
-    def xbg(q):
-        act(("XB", 512 * q, 512 * q + 512), XW, AF.Copy, off=blist(q))
+    def quarter(x, q):
+        return (x, 512 * q, 512 * q + 512)
 
-    def xag(q):
-        gsub(("DD", 512 * q, 512 * q + 512), XW, alist(q), ("XB", 512 * q, 512 * q + 512))
+    def grp(x, q):
+        return (x, 128 * q, 128 * q + 128)
 
-    def zab(q):
-        act(("ZX", 512 * q, 512 * q + 512), ("DD", 512 * q, 512 * q + 512), AF.Abs)
+    def rowbank(q):
+        return ("b%d" % (5 + q // 4), 128 * (q % 4), 128 * (q % 4) + 128)
+
+    E, CP, COL = ("b2", 0, 128), ("b2", 128, 256), ("b2", 264, 272)
+    C2, OO, CNT, SO = ("b0", 256, 264), ("b1", 256, 272), ("b3", 256, 384), ("b3", 384, 392)
+    c1x, u1, u0, X1P = ("b4", 256, 264), ("b4", 264, 272), ("b4", 272, 280), ("b4", 280, 408)
+    XD, XS, X256, XBA = [grp("b7", j) for j in range(4)]
+    FI, SE = grp("FS", 0), grp("FS", 1)
+    F1, X1, U0 = grp("F1X", 0), grp("F1X", 1), grp("F1X", 2)
 
     for t in range(RO):
         last = t == RO - 1
         gat("Cu", SW, "su")
-        gat("G0", SW, ("Cu", 0, 64))
-        if t:
-            ts("sA", "si", ("b2", 256, 257), OP.subtract, 7.0, OP.subtract)
-        ts("C16", "Cu", 1, OP.add)
-        gat("G1", SW, ("Cu", 64, 128))
         for h in range(2):
+            gat("G%d" % h, SW, hf("Cu", h))
             for tab, o in (("DA", 0), ("DB", 64)):
-                for k in range(16):
-                    mm(("b%d" % h, o, o + 64), (tab, 128 * k, 128 * k + 128), ("G%d" % h, k, 1024, 16), k == 0, k == 15)
-        mm(("b3", 256, 384), "I16", "C16", True, True)
-        for m in range(16):
-            o = ("b2", 128 + m, 256, 16)
-            mm(o, ("BM", 128 * m, 128 * m + 128), "sA", True, False)
-            mm(o, "I32", ("C16", m, 128, 16), False, True)
-        cp(("ABT", 0, 128), ("b0", 0, 128))
-        gat(("XB", 0, 512), XW, blist(0))
-        xbg(1)
-        cp(("ABT", 128, 256), ("b1", 0, 128))
-        xag(0)
-        xbg(2)
-        zab(0)
-        xag(1)
-        xbg(3)
-        zab(1)
-        xag(2)
-        zab(2)
-        xag(3)
-        zab(3)
-        if t == 0:
-            act("x256", "xb", AF.Identity, bias=256.0)
-        for h in range(2):
-            for k in range(16):
-                a, b = slm(k)
-                mm(("b2", 64 * h, 64 * h + 64), ("WT", a, b), ("ZX", 1024 * h + k, 1024 * h + 1024, 16), k == 0, k == 15)
+                mms([(("b%d" % h, o, o + 64), grp(tab, k), ("G%d" % h, k, 1024, 16), k == 0, k == 15) for k in range(16)])
+            cp(grp("ABT", h), ("b%d" % h, 0, 128))
+        ts("C16", "Cu", 1, OP.add)
+        act("SL", "TB", AF.Copy, off="su")
+        mms([(CP, "I16", "C16", True, True)])
+        xs = [(E, "I32", "C16", True, False), (E, "IB", "SL", False, not t)]
         if t:
-            x_base()
-            merge_x(t - 1)
-            act("x256", "xb", AF.Identity, bias=256.0)
-        else:
-            tables()
-        ts("ui", U, 16, OP.add)
-        ts("w2", "ui", 255, OP.bitwise_and)
-        tt("sq", "w2", "w2", OP.mult)
-        tt("y", "sq", ("b2", 128, 256), OP.add)
-        ts("yy", "y", 480, OP.bitwise_and)
-        ts("cl", "yy", 0, OP.is_equal)
-        mm(("b3", 0, 128), "TQ", "cl", True, True)
-        mm(("b3", 128, 256), "RC", "cl", True, False)
-        mm(("b3", 128, 256), "I16", "C16", False, True)
+            xs.append((E, "ONB", "FCB", False, True))
+        mms(xs)
+        for q in range(4):
+            if q in VB:
+                gat(quarter("XB", q), XW, blist(q))
+            else:
+                act(quarter("XB", q), XW, AF.Copy, off=blist(q))
+            gsub(quarter("DD", q), XW, alist(q), quarter("XB", q))
+            act(quarter("ZX", q), quarter("DD", q), AF.Abs)
+        for h in range(2):
+            U, Q, R = ("b%d" % h, 128, 192), ("b%d" % (3 + h), 0, 64), ("b%d" % (3 + h), 64, 128)
+            mms([(U, ("WT",) + slm(k), ("ZX", 1024 * h + k, 1024 * h + 1024, 16), k == 0, k == 15) for k in range(16)])
+            ts(hf("ui", h), U, 16, OP.add)
+            ts(hf("w2", h), hf("ui", h), 255, OP.bitwise_and)
+            tt(hf("sq", h), hf("w2", h), hf("w2", h), OP.mult)
+            tt(hf("y", h), hf("sq", h), hf(E, h), OP.add)
+            ts(hf("yy", h), hf("y", h), 480, OP.bitwise_and)
+            ts(hf("cl", h), hf("yy", h), 0, OP.is_equal)
+            mms([(Q, "TQ", hf("cl", h), True, True)])
+            mms([(R, "RC", hf("cl", h), True, False), (R, "I16", hf("C16", h), False, True)])
+            ts(hf(SE, h), Q, 33.0, OP.is_equal)
+            tt(hf("F2", h), hf(SE, h), hf(CP, h), OP.mult)
+            ts(hf(FI, h), Q, 32.0, OP.is_equal)
+            ts(hf(F1, h), R, 6143.0, OP.add, 0.0, OP.min)
         ts("uk", "ui", 2047, OP.bitwise_and)
         ts("ukf", "uk", -16, OP.add)
         ts(U0, "ukf", K0, OP.mult)
-        ts(SE, ("b3", 0, 128), 33.0, OP.is_equal)
+        for h in range(2):
+            FP = ("b%d" % (3 + h), 128, 192)
+            mms([(FP, "I16", hf(FI, h), True, True)])
+            tt(hf(X1, h), FP, hf("ukf", h), OP.mult)
+        listing(C2, "L1", "F2", 128)
+        ts("mN%d" % t, C2, 4097.0, OP.mult, -1.0, OP.add)
+        send(t, "mN%d" % t, "rN%d" % t, "aN%d" % t)
         if not last:
-            tt("F2", SE, ("b3", 256, 384), OP.mult)
-            ts(F1, ("b3", 128, 256), 6143.0, OP.add, 0.0, OP.min)
-            ts(FI, ("b3", 0, 128), 32.0, OP.is_equal)
-            tt(X1, FI, "ukf", OP.mult)
-            msg_n(t)
-            rows()
-            listing(("b4", 0, 24), "L1", "F1X", 384)
-            equal()
-            counts()
-            places()
-            rewrite()
-            pick()
-            mm(("b2", 256, 257), "on32", "fc", True, True)
-            msg_x(t)
-            x_cont()
-            rewrite_end()
-            stand()
-            variables()
-        else:
-            ts(FI, ("b3", 0, 128), 32.0, OP.is_equal)
-            places()
-            tt("F2", SE, ("b3", 256, 384), OP.mult)
-            ts(F1, ("b3", 128, 256), 6143.0, OP.add, 0.0, OP.min)
-            tt(X1, FI, "ukf", OP.mult)
-            pick()
-            listing(("b4", 0, 24), "L1", "F1X", 384)
-            msg_x(t)
-            msg_n(t)
-            rows()
-            variables()
-            dma("y", "oV", [XW], [], T.yv[:], T.ZX[:, 2048:4096])
-            equal()
-            counts()
-            x_cont()
-            rewrite()
-            rewrite_end()
-            stand()
-            x_base()
+            act("sg", C2, AF.Sign, accum_out=("fc", 0, 1))
+            act("FCB", "IB", AF.Identity, scale=0.0, bias=("fc", 0, 1))
+        mms([(COL, F1, "GI", True, True)])
+        act("cola", COL, AF.Copy, scale=-1.0)
+        act("col", COL, AF.Copy)
+        for q in range(8):
+            mms([(rowbank(q), grp("SEL", q), F1, True, True)])
+        for q in range(8):
+            if q < 8 - SQ:
+                ts(grp("EQ", q), rowbank(q), ("col", q, q + 1), OP.is_equal)
+            else:
+                act(grp("EN", q), rowbank(q), AF.Abs, bias=("cola", q, q + 1))
+        act(("EQ", 1024 - 128 * SQ, 1024), ("EN", 1024 - 128 * SQ, 1024), AF.Relu, scale=-1.0, bias=1.0)
+        for h in range(2):
+            mms([((CNT[0], CNT[1] + 16 * q, CNT[1] + 16 * q + 16), grp("EQ", q), "VJ", True, True) for q in range(4 * h, 4 * h + 4)])
+        listing(("b4", 256, 280), "L1", "F1X", 384)
+        ts("c1u", c1x, 2048.0, OP.add)
+        cp("c1h", c1x)
+        gat("Sc", SD, "c1u")
+        tt("lt", CNT, "THR", OP.is_gt)
+        mms([(SO, "lt", "RQ", True, False), (SO, "I16", "c1h", False, True)])
+        mms([(X1P, "I16", X1, True, True)])
+        tt("Sd", "Sc", X1P, OP.add)
+        ts("Sn", "Sd", 2047, OP.bitwise_and)
+        tt("so", SO, "IL", OP.min)
+        ts("sou", "so", 2048.0, OP.add)
+        sca(SD, "sou", "Sn")
+        ts("n1", "si", 5, OP.mult)
+        ts("h1", c1x, 0.0, OP.is_lt, 16777216.0, OP.mult)
+        tt("h2", "h1", c1x, OP.add)
+        tt("n2", "n1", u0, OP.add)
+        ts("n3", "n2", 2047, OP.bitwise_and)
+        tt("sb", "h2", "n3", OP.max)
+        cp("x1", u1)
+        listing(OO, "LK", "FS", 256, ("I16", "CT"))
+        cp("ou", OO)
+        act("z2", ZW, AF.Copy, off=("ou", 8, 16))
+        act("z1", ZW, AF.Copy, off=("ou", 0, 8))
+        mms([(XD, "BF2", SE, True, False), (XD, "IB", "xb", False, False), (XD, "NIB", "z2", False, True)])
+        act("mX%d" % t, XD, AF.Abs, bias=1024.0)
+        send(t, "mX%d" % t, "rX%d" % t, "aX%d" % t)
+        ts("x2", "x1", 15, OP.bitwise_and)
+        tt("x3", "x2", "XO", OP.add)
+        cp("xou", "x3")
+        sca(XW, "xou", "z1")
+        mms([(XS, "BF1", FI, True, False), (XS, "IB", "xb", False, False), (XS, "IB", "z1", False, True)])
+        act(X256, "xb", AF.Identity, bias=256.0)
+        ts("xv", XS, 0.5, OP.mult, 2047.75, OP.add)
+        tt(XBA, "xv", X256, OP.min)
+        if last:
+            dma("y", "oV", [XW], [], T.yv[:], T.ZX[:, 2048:4096], 2 * LOCAL)
             acc = ("b5", 0, 256)
             tt(acc, ("S", 0, 256), ("S", 256, 512), OP.add)
-            for q in range(2, 6):
-                tt(acc, acc, ("S", 256 * q, 256 * q + 256), OP.add)
+            for q in range(2, 8):
+                tt(acc if q < 7 else "yto", acc, ("S", 256 * q, 256 * q + 256), OP.add)
+            dma("y", "oT", ["yto"], [], T.yt[:], T.yto[:], LOCAL)
         tt("se", "sb", "rN%d" % t, OP.max)
         ts("si", "se", 2047, OP.bitwise_and)
-        if not last:
-            cp("su", "si")
-    cp("sf", "si")
-    merge_x(RO - 1)
-    dma("y", "oX", ["xb"], [], T.yx[:], T.xb[:])
-    dma("s", "oS", ["sf"], [], T.ys[:], T.sf[:])
-    tt(acc, acc, ("S", 1536, 1792), OP.add)
-    tt("yto", acc, ("S", 1792, 2048), OP.add)
-    dma("s", "oT", ["yto"], [], T.yt[:], T.yto[:])
-    g.wait_ge(T.sem.sent, sent[0])
-    for s in ("ds0", "dS0", "dw", "dX", "dx0", "oV", "oT", "oS", "oX"):
-        wait("g", {s: 16})
-    finish()
+        cp("sf" if last else "su", "si")
+        if last:
+            dma("s", "oS", ["sf"], [], T.ys[:], T.sf[:], LOCAL)
+        tt("xm", XBA, "rX%d" % t, OP.min)
+        ts("xn", "xm", 255, OP.bitwise_and)
+        cp("xb", "xn")
+    dma("y", "oX", ["xb"], [], T.yx[:], T.xb[:], LOCAL)
+    return emit()

@@ -3,9 +3,10 @@ from concourse.mybir import AluOpType as OP, ActivationFunctionType as AF
 
 N, RO = 8, 3
 NENG = 8
-CH = 32
-VB = (0,)
-SQ = 4
+PIECES = ((0, 16), (16, 32), (32, 64), (64, 96), (96, 112), (112, 128))
+VB = (4,)
+GS = (1, 2)
+SQ = 3
 
 F32, F16, BF, I4, U2 = "float32", "float16", "bfloat16", "int32", "uint16"
 SCRATCH = {}
@@ -21,11 +22,11 @@ _sb(BF, ZX=4096, xb=128)
 _sb(U2, su=8)
 _sb(I4, cp=1, cq=4)
 _sb(F32, cI=144, cf=16, tq=128, rc=128, blk=128, mk=128, l256=16, rm=16, gm=8, ex=16, z16=16, THR=128, IL=8, XO=8, il0=8, pf=16)
-_sb(F16, I16=128, P16=128, I32=128, L1=144, LK=144, DA=2048, DB=2048, BN=128, SEL=1024, on16=128, TQ=128, RC=128,
+_sb(F16, I16=128, P16=128, I32=128, N16=128, L1=144, LK=144, DA=2048, DB=2048, BN=128, SEL=1024, on16=128, TQ=128, RC=128,
     BO=128, BF1=128, BF2=128, RQ=8, GI=8, CT=16)
 _sb(BF, TB=2048, SL=128, FCB=128, ONB=128, IB=128, NIB=128, WT=144, VJ=16)
 _sb(U2, Cu=128, ABT=256, ou=16, c1u=8, sou=8, xou=8)
-_sb(F16, C16=128, G0=1024, G1=1024, cl=128, ukf=128, FS=256, F1X=384, F2=128, lt=128, c1h=8)
+_sb(F16, C16=128, G0=1024, G1=1024, cl=128, FS=256, F1X=384, F2=128, lt=128, c1h=8)
 _sb(BF, XB=2048, DD=2048, EQ=1024, EN=1024, z1=128, z2=128, sg=8)
 _sb(I4, ui=128, w2=128, sq=128, y=128, yy=128, uk=128, Sc=128, Sd=128, Sn=128, x1=8, x2=8, x3=8, n2=8, n3=8, se=8, xv=128,
     xm=128, xn=128)
@@ -40,6 +41,16 @@ for _b in PSUM:
     SCRATCH[_b] = ("psum", [128, 512], F32)
 
 CYC, PECYC, GATH, SCAT, WAKE, LOCAL, FLIGHT = 0.0012, 0.0005, 2.0, 3.8, 0.06, 2.0, 3.0
+ORDER = (
+    "000105270403071t020m0l0k0o080n28061v0b0s242s0q2k0p220g1l0v1b131s0t152p1n191r171j0r2t251c0w181m1o0u1a160y1i5t14121p101u1k2123"
+    "0z1w11261x1f1h1d1g1e0x2v0e382w090h0f0i0j0a312x0c2z0d2y323e3h301q333f353b343i3g3k363c3n3j3l3q3d3o3m3t3r3p3u373s1y3v39293a2046"
+    "3w2a1z3x472h3y484j494k4a3z2b4b412g402f4c42454e444d432d4l4f4h2e4g4i2n4p4m2m2l2i2r2u544v534q4n4y2o4w522c4x554r4o514t2q4z505a5h"
+    "4u4s2j585b56575d605i595c5j5k5f5e5n615u5w5z625o5g5x5v635p645l685y655m695q6a666c5r6b676d5s6e6g6f6h6i9k6z6m6n6t6o6q6p6s75786r6y"
+    "6u6j766w726v797071777b6x737e7a7c747h7k7f7d7i7g6k7j7l6l7m7n7x7o7p7y7q7z8a7r7s807w7v818b827t837u8c858d84868988878p8t8e8g8f8m8r"
+    "8u8h8o8w8v8n8q8i8k8s91988l8x8j8y928z9r93909a94999b9e95969q9n9f9o9z979g9l9c9ma09d9s9p9h9ua19i9j9t9va29w9xa3a79ya4a8a9a5aqada6"
+    "aeakafahagajawazaiaaalaxanatamb0b8b2aob5aub1b3avayb6b4bbb9b7apbcbaabarasbdd9acbebobfbgbpbhbqc1bibjbrc2bsbmbnbtbkbublc3bwc4bv"
+    "c0bzbxcjcickbyc5dgc6cbcgcedhcdcfclccchdicxcqcoctcndkcmcrcyc7czcscpd0dld3cuc8cvdmd4dac9dndcd5djcwdfcadbddd1dsdoded2dpdtd6dqd7"
+    "drd8dwdudxdvdydze0e9e1eae5e2ebe6e3ece7e4e8")
 
 
 def make_plan(g, T):
@@ -135,7 +146,7 @@ def make_plan(g, T):
                 for k, m in event[(src, need[src])].items():
                     clock[q][k] = max(clock[q].get(k, 0), m)
 
-        seq = order()
+        seq = [36 * int(ORDER[i], 36) + int(ORDER[i + 1], 36) for i in range(0, len(ORDER), 2)] or order()
         for i in seq:
             x = nodes[i]
             q = x["q"]
@@ -318,6 +329,7 @@ def rank_program(g, core, T, topo):
     ts("I32", "I16", 32.0, OP.mult)
     ts("IB", "I16", 1.0, OP.mult)
     fill("ONB", 32.0)
+    ts("N16", "I16", -16.0, OP.mult)
     ts(PG16, PG, 16.0, OP.add)
     cp(WC, "wi")
     ts("WT", "cI", PG16, OP.is_equal, WC, OP.mult)
@@ -342,10 +354,10 @@ def rank_program(g, core, T, topo):
     ts("RQ", "gm", 4096.0, OP.mult)
     ts("IL", "il0", PM, OP.add)
     ts("XO", ("l256", 0, 8), XOC, OP.add)
-    ts("NIB", "I16", -1.0, OP.mult)
+    act("NIB", "IB", AF.Copy, scale=-1.0)
     ts("BF2", "BN", 32.0, OP.mult)
     ts("BF1", "BN", 192.0, OP.mult)
-    cp("VJ", "z16")
+    act("VJ", "pf", AF.Exp, scale=-math.log(2.0), bias=60.0 * math.log(2.0))
     ts(("z16", 0, 1), ("z16", 0, 1), 2.5, OP.mult)
     ts("THR", "THR", ("z16", 0, 1), OP.max)
 
@@ -371,16 +383,13 @@ def rank_program(g, core, T, topo):
             x = (x, 0, 128)
         return (x[0], x[1] + 64 * h, x[1] + 64 * h + 64)
 
-    def alist(q):
-        a = 128 * (q // 2) + CH * (q % 2)
-        return ("ABT", a, a + CH)
+    def ablist(q, o):
+        st, en = PIECES[q]
+        a = 128 * (st // 64) + 64 * o + st % 64
+        return ("ABT", a, a + en - st)
 
-    def blist(q):
-        a = 128 * (q // 2) + 64 + CH * (q % 2)
-        return ("ABT", a, a + CH)
-
-    def quarter(x, q):
-        return (x, 512 * q, 512 * q + 512)
+    def piece(x, q):
+        return (x, 16 * PIECES[q][0], 16 * PIECES[q][1])
 
     def grp(x, q):
         return (x, 128 * q, 128 * q + 128)
@@ -399,10 +408,12 @@ def rank_program(g, core, T, topo):
         last = t == RO - 1
         gat("Cu", SW, "su")
         for h in range(2):
-            gat("G%d" % h, SW, hf("Cu", h))
-            for tab, o in (("DA", 0), ("DB", 64)):
-                mms([(("b%d" % h, o, o + 64), grp(tab, k), ("G%d" % h, k, 1024, 16), k == 0, k == 15) for k in range(16)])
-            cp(grp("ABT", h), ("b%d" % h, 0, 128))
+            w = 64 // GS[h]
+            for j in range(GS[h]):
+                gat(("G%d" % h, 16 * w * j, 16 * w * (j + 1)), SW, ("Cu", 64 * h + w * j, 64 * h + w * (j + 1)))
+            for tab, bk, o in (("DB", "b%d" % (5 + h), 64), ("DA", "b%d" % h, 0)):
+                mms([((bk, 0, 64), grp(tab, k), ("G%d" % h, k, 1024, 16), k == 0, k == 15) for k in range(16)])
+                cp(("ABT", 128 * h + o, 128 * h + o + 64), (bk, 0, 64))
         ts("C16", "Cu", 1, OP.add)
         act("SL", "TB", AF.Copy, off="su")
         mms([(CP, "I16", "C16", True, True)])
@@ -410,13 +421,13 @@ def rank_program(g, core, T, topo):
         if t:
             xs.append((E, "ONB", "FCB", False, True))
         mms(xs)
-        for q in range(4):
+        for q in range(len(PIECES)):
             if q in VB:
-                gat(quarter("XB", q), XW, blist(q))
+                gat(piece("XB", q), XW, ablist(q, 1))
             else:
-                act(quarter("XB", q), XW, AF.Copy, off=blist(q))
-            gsub(quarter("DD", q), XW, alist(q), quarter("XB", q))
-            act(quarter("ZX", q), quarter("DD", q), AF.Abs)
+                act(piece("XB", q), XW, AF.Copy, off=ablist(q, 1))
+            gsub(piece("DD", q), XW, ablist(q, 0), piece("XB", q))
+            act(piece("ZX", q), piece("DD", q), AF.Abs)
         for h in range(2):
             U, Q, R = ("b%d" % h, 128, 192), ("b%d" % (3 + h), 0, 64), ("b%d" % (3 + h), 64, 128)
             mms([(U, ("WT",) + slm(k), ("ZX", 1024 * h + k, 1024 * h + 1024, 16), k == 0, k == 15) for k in range(16)])
@@ -433,12 +444,11 @@ def rank_program(g, core, T, topo):
             ts(hf(FI, h), Q, 32.0, OP.is_equal)
             ts(hf(F1, h), R, 6143.0, OP.add, 0.0, OP.min)
         ts("uk", "ui", 2047, OP.bitwise_and)
-        ts("ukf", "uk", -16, OP.add)
-        ts(U0, "ukf", K0, OP.mult)
+        ts(U0, "uk", K0, OP.mult)
         for h in range(2):
             FP = ("b%d" % (3 + h), 128, 192)
             mms([(FP, "I16", hf(FI, h), True, True)])
-            tt(hf(X1, h), FP, hf("ukf", h), OP.mult)
+            tt(hf(X1, h), FP, hf("uk", h), OP.mult)
         listing(C2, "L1", "F2", 128)
         ts("mN%d" % t, C2, 4097.0, OP.mult, -1.0, OP.add)
         send(t, "mN%d" % t, "rN%d" % t, "aN%d" % t)
@@ -464,13 +474,13 @@ def rank_program(g, core, T, topo):
         gat("Sc", SD, "c1u")
         tt("lt", CNT, "THR", OP.is_gt)
         mms([(SO, "lt", "RQ", True, False), (SO, "I16", "c1h", False, True)])
-        mms([(X1P, "I16", X1, True, True)])
+        mms([(X1P, "I16", X1, True, False), (X1P, "N16", FI, False, True)])
         tt("Sd", "Sc", X1P, OP.add)
         ts("Sn", "Sd", 2047, OP.bitwise_and)
         tt("so", SO, "IL", OP.min)
         ts("sou", "so", 2048.0, OP.add)
         sca(SD, "sou", "Sn")
-        ts("n1", "si", 5, OP.mult)
+        ts("n1", "si", 5, OP.mult, -16, OP.add)
         ts("h1", c1x, 0.0, OP.is_lt, 16777216.0, OP.mult)
         tt("h2", "h1", c1x, OP.add)
         tt("n2", "n1", u0, OP.add)

import math
from concourse.mybir import AluOpType as OP, ActivationFunctionType as AF

N, RO = 8, 3
NENG = 8
PIECES = ((0, 16), (16, 32), (32, 64), (64, 96), (96, 112), (112, 128))
VB = (4,)
GS = (1, 2)
SQ = 3

F32, F16, BF, I4, U2 = "float32", "float16", "bfloat16", "int32", "uint16"
SCRATCH = {}


def _sb(dtype, **bufs):
    for name in bufs:
        SCRATCH[name] = ("sbuf", [128, bufs[name]], dtype)


_sb(I4, S=2176, si=8, wi=1)
_sb(BF, ZX=4096, xb=128)
_sb(U2, su=8)
_sb(I4, cp=1, cq=4)
_sb(F32, cI=144, cf=16, tq=128, rc=128, blk=128, mk=128, l256=16, rm=16, gm=8, ex=16, z16=16, THR=128, IL=8, XO=8, il0=8, pf=16)
_sb(F16, I16=128, P16=128, I32=128, N16=128, L1=144, LK=144, DA=2048, DB=2048, BN=128, SEL=1024, on16=128, TQ=128, RC=128,
    BO=128, BF1=128, BF2=128, RQ=8, GI=8, CT=16)
_sb(BF, TB=2048, SL=128, FCB=128, ONB=128, IB=128, NIB=128, WT=144, VJ=16)
_sb(U2, Cu=128, ABT=256, ou=16, c1u=8, sou=8, xou=8)
_sb(F16, C16=128, G0=1024, G1=1024, cl=128, FS=256, F1X=384, F2=128, lt=128, c1h=8)
_sb(BF, XB=2048, DD=2048, EQ=1024, EN=1024, z1=128, z2=128, sg=8)
_sb(I4, ui=128, w2=128, sq=128, y=128, yy=128, uk=128, Sc=128, Sd=128, Sn=128, x1=8, x2=8, x3=8, n2=8, n3=8, se=8, xv=128,
    xm=128, xn=128)
_sb(F32, col=8, cola=8, so=8, n1=8, h1=8, h2=8, sb=8, fc=1, sf=8, yto=256)
SEMAPHORES = ["qv", "qs", "qp", "qg", "dS0", "dX", "dx0", "dw", "ds0", "oV", "oT", "oX", "oS", "sent"]
for _t in range(RO):
    _sb(F32, **{"mN%d" % _t: 8, "rN%d" % _t: 8})
    _sb(BF, **{"mX%d" % _t: 128, "rX%d" % _t: 128})
    SEMAPHORES += ["aN%d" % _t, "aX%d" % _t]
PSUM = ["b%d" % _b for _b in range(8)]
for _b in PSUM:
    SCRATCH[_b] = ("psum", [128, 512], F32)

CYC, PECYC, GATH, SCAT, WAKE, LOCAL, FLIGHT = 0.0012, 0.0005, 2.0, 3.8, 0.06, 2.0, 3.0
ORDER = (
    "000105270403071t020m0l0k0o080n28061v0b0s242s0q2k0p220g1l0v1b131s0t152p1n191r171j0r2t251c0w181m1o0u1a160y1i5t14121p101u1k2123"
    "0z1w11261x1f1h1d1g1e0x2v0e382w090h0f0i0j0a312x0c2z0d2y323e3h301q333f353b343i3g3k363c3n3j3l3q3d3o3m3t3r3p3u373s1y3v39293a2046"
    "3w2a1z3x472h3y484j494k4a3z2b4b412g402f4c42454e444d432d4l4f4h2e4g4i2n4p4m2m2l2i2r2u544v534q4n4y2o4w522c4x554r4o514t2q4z505a5h"
    "4u4s2j585b56575d605i595c5j5k5f5e5n615u5w5z625o5g5x5v635p645l685y655m695q6a666c5r6b676d5s6e6g6f6h6i9k6z6m6n6t6o6q6p6s75786r6y"
    "6u6j766w726v797071777b6x737e7a7c747h7k7f7d7i7g6k7j7l6l7m7n7x7o7p7y7q7z8a7r7s807w7v818b827t837u8c858d84868988878p8t8e8g8f8m8r"
    "8u8h8o8w8v8n8q8i8k8s91988l8x8j8y928z9r93909a94999b9e95969q9n9f9o9z979g9l9c9ma09d9s9p9h9ua19i9j9t9va29w9xa3a79ya4a8a9a5aqada6"
    "aeakafahagajawazaiaaalaxanatamb0b8b2aob5aub1b3avayb6b4bbb9b7apbcbaabarasbdd9acbebobfbgbpbhbqc1bibjbrc2bsbmbnbtbkbublc3bwc4bv"
    "c0bzbxcjcickbyc5dgc6cbcgcedhcdcfclccchdicxcqcoctcndkcmcrcyc7czcscpd0dld3cuc8cvdmd4dac9dndcd5djcwdfcadbddd1dsdoded2dpdtd6dqd7"
    "drd8dwdudxdvdydze0e9e1eae5e2ebe6e3ece7e4e8")


def make_plan(g, T):
    eng = {"v": g.vector, "s": g.scalar, "p": g.tensor, "g": g, "y": g.sync}
    qsem = {"v": "qv", "s": "qs", "p": "qp", "g": "qg"}
    nodes = []
    hist = {}

    def rng(x):
        return (x, 0, T[x].shape[1]) if isinstance(x, str) else x

    def add(q, rd, wr, fns, dur, sem=None, inc=1, lat=0.0, after=None):
        i = len(nodes)
        rd = [rng(x) for x in rd]
        wr = [rng(x) for x in wr]
        pred = {}
        for acc, isw in ((rd, False), (wr, True)):
            for name, a, b in acc:
                for (a0, b0, w0, j) in hist.get(name, []):
                    over = a < b0 and a0 < b and (isw or w0)
                    if name in PSUM:
                        if nodes[j]["q"] != q or (over and q != "p"):
                            pred[j] = True
                        elif over:
                            pred.setdefault(j, False)
                    elif over:
                        pred[j] = True
        if after is not None:
            pred[after] = False
        nodes.append({"q": q, "fns": fns, "dur": dur, "sem": sem, "inc": inc, "lat": lat, "pred": pred, "i": i})
        for name, a, b in wr:
            keep = [h for h in hist.get(name, []) if not (a <= h[0] and h[1] <= b and h[3] in pred)]
            hist[name] = keep + [(a, b, True, i)]
        for name, a, b in rd:
            hist[name] = hist.get(name, []) + [(a, b, False, i)]
        return i

    def order():
        n = len(nodes)
        succ = [[] for _ in nodes]
        for x in nodes:
            for j, w in x["pred"].items():
                succ[j].append((x["i"], w))
        prio = [0.0] * n
        for i in range(n - 1, -1, -1):
            x = nodes[i]
            best = max([prio[j] + (WAKE if w else 0.0) for j, w in succ[i]] + [0.0])
            prio[i] = best + x["dur"] + x["lat"]
        left = [len(x["pred"]) for x in nodes]
        ready = [0.0] * n
        free = {}
        avail = {}
        for x in nodes:
            if not left[x["i"]]:
                avail.setdefault(x["q"], []).append(x["i"])
        out = []
        while any(avail.values()):
            pick = None
            for q in avail:
                if not avail[q]:
                    continue
                fr = free.get(q, 0.0) if q != "n" else 0.0
                t0 = min(max(fr, ready[i]) for i in avail[q])
                c = [i for i in avail[q] if max(fr, ready[i]) <= t0 + 0.02]
                i = max(c, key=lambda k: prio[k])
                t1 = max(fr, ready[i])
                if pick is None or t1 < pick[0]:
                    pick = (t1, i, q)
            t1, i, q = pick
            avail[q].remove(i)
            x = nodes[i]
            end = t1 + x["dur"]
            free[q] = end
            out.append(i)
            for j, w in succ[i]:
                ready[j] = max(ready[j], end + x["lat"] + (WAKE if w else 0.0))
                left[j] -= 1
                if not left[j]:
                    avail.setdefault(nodes[j]["q"], []).append(j)
        return out

    def emit():
        count = {}
        clock = dict((q, {}) for q in eng)
        event = {}
        where = {}

        def wait(q, need):
            for src in sorted(need):
                if not any(event[(o, need[o])].get(src, 0) >= need[src] for o in need if o != src):
                    eng[q].wait_ge(T.sem[qsem.get(src, src)], need[src])
            for src in need:
                for k, m in event[(src, need[src])].items():
                    clock[q][k] = max(clock[q].get(k, 0), m)

        seq = [36 * int(ORDER[i], 36) + int(ORDER[i + 1], 36) for i in range(0, len(ORDER), 2)] or order()
        for i in seq:
            x = nodes[i]
            q = x["q"]
            if q == "n":
                where[i] = (x["sem"], x["inc"])
                event[where[i]] = {x["sem"]: x["inc"]}
                continue
            need = {}
            for j, w in x["pred"].items():
                if w:
                    src, n = where[j]
                    if n > clock[q].get(src, 0):
                        need[src] = max(need.get(src, 0), n)
            wait(q, need)
            if x["sem"] is None:
                for fn in x["fns"]:
                    fn(eng[q]).then_inc(T.sem[qsem[q]], 1)
                    count[q] = count.get(q, 0) + 1
                where[i] = (q, count[q])
            else:
                for fn in x["fns"]:
                    ins = fn(eng[q])
                    if x["sem"] != "sent":
                        ins.then_inc(T.sem[x["sem"]], 16)
                where[i] = (x["sem"], x["inc"])
            ev = dict(clock[q])
            ev[where[i][0]] = where[i][1]
            event[where[i]] = ev
        for x in nodes:
            if x["sem"] is not None and x["sem"] != "sent" and x["q"] != "n" and x["inc"] > clock["g"].get(x["sem"], 0):
                wait("g", {x["sem"]: x["inc"]})
        g.wait_ge(T.sem.sent, sum(x["inc"] for x in nodes if x["sem"] == "sent"))
        for q in ("v", "s", "p", "g"):
            if count[q] > clock["g"].get(q, 0):
                wait("g", {q: count[q]})
        return nodes, seq
    return add, emit


def rank_program(g, core, T, topo):
    rank = T.rank_of(core)
    if rank is None:
        return
    add, emit = make_plan(g, T)

    def cols(x):
        if isinstance(x, str):
            n = T[x].shape[1]
            return T[x][:, 0:n], (x, 0, n)
        name, a, b = x[:3]
        if len(x) == 4:
            return T[name][:, a:b:x[3]], (name, a, b)
        return T[name][:, a:b], (name, a, b)

    def width(x):
        r = cols(x)[1]
        return (r[2] - r[1]) // (x[3] if len(x) == 4 and not isinstance(x, str) else 1)

    def buf(x):
        return x if isinstance(x, str) else x[0]

    def small(*xs):
        return all(SCRATCH[buf(x)][2] in (F16, BF, U2) for x in xs)

    def vec(ins, out, fn, cyc):
        add("v", [cols(x)[1] for x in ins], [cols(out)[1]], [fn], CYC * max(64, cyc))

    def ts(out, in0, s1, op0, s2=None, op1=None):
        o, i = cols(out)[0], cols(in0)[0]
        rd = [in0] + [x for x in (s1, s2) if isinstance(x, tuple)]
        s1 = cols(s1)[0] if isinstance(s1, tuple) else s1
        s2 = cols(s2)[0] if isinstance(s2, tuple) else s2
        if op1 is None:
            fn = lambda e: e.tensor_scalar(o, i, s1, None, op0)
        else:
            fn = lambda e: e.tensor_scalar(o, i, s1, s2, op0, op1)
        vec(rd, out, fn, width(out) * (0.5 if small(out, in0) else 1))

    def tt(out, in0, in1, op):
        o, a, b = cols(out)[0], cols(in0)[0], cols(in1)[0]
        ps = buf(in0) in PSUM or buf(in1) in PSUM
        vec([in0, in1], out, lambda e: e.tensor_tensor(o, a, b, op), width(out) * (1 if ps else 2))

    def cp(out, in0):
        o, a = cols(out)[0], cols(in0)[0]
        vec([in0], out, lambda e: e.tensor_copy(o, a), width(out) * (0.5 if small(out, in0) else 1))

    def gat(out, win, off):
        o, w, f = cols(out)[0], cols(win)[0], cols(off)[0]
        vec([win, off], out, lambda e: e.tensor_copy(o, w.indirect(f)), 50 + GATH * width(out))

    def gsub(out, win, off, in1):
        o, w, f, b = cols(out)[0], cols(win)[0], cols(off)[0], cols(in1)[0]
        vec([win, off, in1], out, lambda e: e.tensor_tensor(o, w.indirect(f), b, OP.subtract), 50 + GATH * width(out))

    def sca(win, off, in0):
        w, f, a = cols(win)[0], cols(off)[0], cols(in0)[0]
        vec([off, in0], win, lambda e: e.tensor_copy(w.indirect(f), a), 50 + SCAT * width(in0))

    def fill(out, v):
        o = cols(out)[0]
        vec([], out, lambda e: e.memset(o, v), width(out))

    def act(out, in0, func, off=None, **kw):
        o, a = cols(out)[0], cols(in0)[0]
        rd, wr, kk = [cols(in0)[1]], [cols(out)[1]], {}
        for k, v in kw.items():
            if isinstance(v, tuple):
                v, r = cols(v)
                (wr if k == "accum_out" else rd).append(r)
            kk[k] = v
        if off is not None:
            f, rf = cols(off)
            a = a.indirect(f)
            rd.append(rf)
        add("s", rd, wr, [lambda e: e.activation(o, a, func, **kk)], CYC * (65 + width(out) * (GATH if off is not None else 1)))

    def one(x):
        o, a, b = cols(x[0])[0], cols(x[1])[0], cols(x[2])[0]
        return lambda e: e.matmul(o, a, b, x[3], x[4])

    def mms(xs):
        rd = sorted(set(cols(x[1])[1] for x in xs) | set(cols(x[2])[1] for x in xs))
        wr = sorted(set(cols(x[0])[1] for x in xs))
        add("p", rd, wr, [one(x) for x in xs], sum(max(64, width(x[0])) * PECYC for x in xs))

    def iota(out, pattern, base, cm, flag=True):
        o = cols(out)[0]
        if flag:
            fn = lambda e: e.iota(o, pattern, base, cm, allow_small_or_imprecise_dtypes=True)
        else:
            fn = lambda e: e.iota(o, pattern, base, cm)
        add("g", [], [cols(out)[1]], [fn], 0.13 + 2 * CYC * width(out))

    def sel(out, op, v):
        o, ro = cols(out)
        add("g", [ro], [ro], [lambda e: e.affine_select(o, o, [[1, 128]], op, v, 0, -1)], 0.17 + 2 * CYC * width(out))

    def dma(q, s, rd, wr, out, in_, us):
        add(q, rd, wr, [lambda e: e.dma_start(out, in_)], 0.1, sem=s, inc=16, lat=us)

    SW, SD, XW, ZW = ("S", 0, 2048), ("S", 0, 2176), ("ZX", 2048, 4096), ("ZX", 0, 4096)

    dma("s", "ds0", [], ["si"], T.si[:], T.s0[:], LOCAL)
    dma("y", "dS0", [], [SW], T.S[:, 0:2048], T.stm[:], 6.0)
    dma("s", "dw", [], ["wi"], T.wi[:], T.wt[:], LOCAL)
    dma("y", "dX", [], [XW], T.ZX[:, 2048:4096], T.vx[:], 9.0)
    dma("s", "dx0", [], ["xb"], T.xb[:], T.x0[:], LOCAL)

    iota("cp", [[1, 1]], 0, 1, False)
    iota("pf", [[0, 16]], 0, 1)
    iota("cI", [[1, 144]], 0, 0)
    iota("ex", [[1, 16]], 0, 0)
    iota("blk", [[16, 8], [0, 16]], 0, 0)
    iota("tq", [[0, 128]], 1, 0)
    iota("rc", [[0, 128]], 8192, 0)
    for name, own in (("tq", 32.0), ("rc", -8192.0)):
        sel(name, OP.is_gt, 0.0)
        sel(name, OP.not_equal, own)
    iota("TB", [[0, 128], [-32, 16]], 224, 0)
    iota("mk", [[0, 8], [1, 16]], 0, 0)
    iota("il0", [[16, 8]], 0, 0)
    iota("l256", [[0, 2], [256, 8]], 0, 0)
    P = ("pf", 0, 1)
    PX, PM, PG, PG16, KM, K0, WC, CTC, XOC = [("cf", j, j + 1) for j in range(9)]
    ts(("cq", 0, 1), "cp", 15, OP.bitwise_and)
    ts(("cq", 1, 2), "cp", 112, OP.bitwise_and)
    ts(("cq", 2, 3), "cp", 1, OP.bitwise_and)
    cp(("cf", 1, 3), ("cq", 0, 2))
    ts(PX, ("cq", 2, 3), -2, OP.mult, 1, OP.add)
    tt(PX, PX, P, OP.add)
    ts("I16", ("cI", 0, 128), P, OP.is_equal)
    ts("P16", ("cI", 0, 128), PX, OP.is_equal)
    ts("rm", "ex", PM, OP.is_equal)
    for k in range(16):
        ts(("DA", 128 * k, 128 * k + 128), "I16", ("rm", k, k + 1), OP.mult)
        ts(("DB", 128 * k, 128 * k + 128), "P16", ("rm", k ^ 1, (k ^ 1) + 1), OP.mult)
    cp("su", "si")
    ts("BN", "blk", PG, OP.is_equal, -32.0, OP.mult)
    ts("I32", "I16", 32.0, OP.mult)
    ts("IB", "I16", 1.0, OP.mult)
    fill("ONB", 32.0)
    ts("N16", "I16", -16.0, OP.mult)
    ts(PG16, PG, 16.0, OP.add)
    cp(WC, "wi")
    ts("WT", "cI", PG16, OP.is_equal, WC, OP.mult)
    ts("BO", "BN", -0.03125, OP.mult)
    tt("TQ", "tq", "BO", OP.mult)
    tt("RC", "rc", "BO", OP.mult)
    ts(KM, PM, -2048.0, OP.add)
    ts(K0, PM, 0.0, OP.is_equal)
    ts(CTC, PM, 16.0, OP.mult, 2048.0, OP.add)
    ts(XOC, PM, 16.0, OP.mult)
    ts("L1", "cI", PG16, OP.is_equal)
    ts("LK", "cI", PG16, OP.is_equal, KM, OP.mult)
    fill(("S", 2048, 2176), 0)
    ts("on16", ("cI", 0, 128), 0.0, OP.mult, 1.0, OP.add)
    ts("gm", "il0", PG, OP.is_equal)
    for q in range(8):
        ts(("SEL", 128 * q, 128 * q + 128), "on16", ("gm", q, q + 1), OP.mult)
    cp("GI", "gm")
    ts("CT", "l256", CTC, OP.add)
    act("z16", "pf", AF.Exp, scale=-math.log(2.0), bias=60.0 * math.log(2.0))
    ts("THR", "mk", PM, OP.not_equal, 2.0 ** 97, OP.mult)
    ts("RQ", "gm", 4096.0, OP.mult)
    ts("IL", "il0", PM, OP.add)
    ts("XO", ("l256", 0, 8), XOC, OP.add)
    act("NIB", "IB", AF.Copy, scale=-1.0)
    ts("BF2", "BN", 32.0, OP.mult)
    ts("BF1", "BN", 192.0, OP.mult)
    act("VJ", "pf", AF.Exp, scale=-math.log(2.0), bias=60.0 * math.log(2.0))
    ts(("z16", 0, 1), ("z16", 0, 1), 2.5, OP.mult)
    ts("THR", "THR", ("z16", 0, 1), OP.max)

    def slm(m):
        return 16 - m, 144 - m

    def listing(out, tab, rhs, wid, more=None):
        xs = [(out, (tab,) + slm(m), (rhs, m, wid, 16), m == 0, more is None and m == 15) for m in range(16)]
        if more is not None:
            xs.append((out, more[0], more[1], False, True))
        mms(xs)

    def send(t, src, dst_buf, sem):
        to = T.cores[(rank + 1 + t % (N - 1)) % N]
        rid, pid = topo.addr(to)[:2]
        mask = sum(1 << e for e in topo.engines(core, to)[:NENG])
        i = add("g", [src], [], [lambda e: e.remote_dma(T[dst_buf][:], T[src][:], T.sem[sem], T.sem.sent, pid, rid, mask)], 0.3,
                sem="sent", inc=NENG)
        add("n", [], [dst_buf], [], 0.0, sem=sem, inc=NENG, lat=FLIGHT, after=i)

    def hf(x, h):
        if isinstance(x, str):
            x = (x, 0, 128)
        return (x[0], x[1] + 64 * h, x[1] + 64 * h + 64)

    def ablist(q, o):
        st, en = PIECES[q]
        a = 128 * (st // 64) + 64 * o + st % 64
        return ("ABT", a, a + en - st)

    def piece(x, q):
        return (x, 16 * PIECES[q][0], 16 * PIECES[q][1])

    def grp(x, q):
        return (x, 128 * q, 128 * q + 128)

    def rowbank(q):
        return ("b%d" % (5 + q // 4), 128 * (q % 4), 128 * (q % 4) + 128)

    E, CP, COL = ("b2", 0, 128), ("b2", 128, 256), ("b2", 264, 272)
    C2, OO, CNT, SO = ("b0", 256, 264), ("b1", 256, 272), ("b3", 256, 384), ("b3", 384, 392)
    c1x, u1, u0, X1P = ("b4", 256, 264), ("b4", 264, 272), ("b4", 272, 280), ("b4", 280, 408)
    XD, XS, X256, XBA = [grp("b7", j) for j in range(4)]
    FI, SE = grp("FS", 0), grp("FS", 1)
    F1, X1, U0 = grp("F1X", 0), grp("F1X", 1), grp("F1X", 2)

    for t in range(RO):
        last = t == RO - 1
        gat("Cu", SW, "su")
        for h in range(2):
            w = 64 // GS[h]
            for j in range(GS[h]):
                gat(("G%d" % h, 16 * w * j, 16 * w * (j + 1)), SW, ("Cu", 64 * h + w * j, 64 * h + w * (j + 1)))
            for tab, bk, o in (("DB", "b%d" % (5 + h), 64), ("DA", "b%d" % h, 0)):
                mms([((bk, 0, 64), grp(tab, k), ("G%d" % h, k, 1024, 16), k == 0, k == 15) for k in range(16)])
                cp(("ABT", 128 * h + o, 128 * h + o + 64), (bk, 0, 64))
        ts("C16", "Cu", 1, OP.add)
        act("SL", "TB", AF.Copy, off="su")
        mms([(CP, "I16", "C16", True, True)])
        xs = [(E, "I32", "C16", True, False), (E, "IB", "SL", False, not t)]
        if t:
            xs.append((E, "ONB", "FCB", False, True))
        mms(xs)
        for q in range(len(PIECES)):
            if q in VB:
                gat(piece("XB", q), XW, ablist(q, 1))
            else:
                act(piece("XB", q), XW, AF.Copy, off=ablist(q, 1))
            gsub(piece("DD", q), XW, ablist(q, 0), piece("XB", q))
            act(piece("ZX", q), piece("DD", q), AF.Abs)
        for h in range(2):
            U, Q, R = ("b%d" % h, 128, 192), ("b%d" % (3 + h), 0, 64), ("b%d" % (3 + h), 64, 128)
            mms([(U, ("WT",) + slm(k), ("ZX", 1024 * h + k, 1024 * h + 1024, 16), k == 0, k == 15) for k in range(16)])
            ts(hf("ui", h), U, 16, OP.add)
            ts(hf("w2", h), hf("ui", h), 255, OP.bitwise_and)
            tt(hf("sq", h), hf("w2", h), hf("w2", h), OP.mult)
            tt(hf("y", h), hf("sq", h), hf(E, h), OP.add)
            ts(hf("yy", h), hf("y", h), 480, OP.bitwise_and)
            ts(hf("cl", h), hf("yy", h), 0, OP.is_equal)
            mms([(Q, "TQ", hf("cl", h), True, True)])
            mms([(R, "RC", hf("cl", h), True, False), (R, "I16", hf("C16", h), False, True)])
            ts(hf(SE, h), Q, 33.0, OP.is_equal)
            tt(hf("F2", h), hf(SE, h), hf(CP, h), OP.mult)
            ts(hf(FI, h), Q, 32.0, OP.is_equal)
            ts(hf(F1, h), R, 6143.0, OP.add, 0.0, OP.min)
        ts("uk", "ui", 2047, OP.bitwise_and)
        ts(U0, "uk", K0, OP.mult)
        for h in range(2):
            FP = ("b%d" % (3 + h), 128, 192)
            mms([(FP, "I16", hf(FI, h), True, True)])
            tt(hf(X1, h), FP, hf("uk", h), OP.mult)
        listing(C2, "L1", "F2", 128)
        ts("mN%d" % t, C2, 4097.0, OP.mult, -1.0, OP.add)
        send(t, "mN%d" % t, "rN%d" % t, "aN%d" % t)
        if not last:
            act("sg", C2, AF.Sign, accum_out=("fc", 0, 1))
            act("FCB", "IB", AF.Identity, scale=0.0, bias=("fc", 0, 1))
        mms([(COL, F1, "GI", True, True)])
        act("cola", COL, AF.Copy, scale=-1.0)
        act("col", COL, AF.Copy)
        for q in range(8):
            mms([(rowbank(q), grp("SEL", q), F1, True, True)])
        for q in range(8):
            if q < 8 - SQ:
                ts(grp("EQ", q), rowbank(q), ("col", q, q + 1), OP.is_equal)
            else:
                act(grp("EN", q), rowbank(q), AF.Abs, bias=("cola", q, q + 1))
        act(("EQ", 1024 - 128 * SQ, 1024), ("EN", 1024 - 128 * SQ, 1024), AF.Relu, scale=-1.0, bias=1.0)
        for h in range(2):
            mms([((CNT[0], CNT[1] + 16 * q, CNT[1] + 16 * q + 16), grp("EQ", q), "VJ", True, True) for q in range(4 * h, 4 * h + 4)])
        listing(("b4", 256, 280), "L1", "F1X", 384)
        ts("c1u", c1x, 2048.0, OP.add)
        cp("c1h", c1x)
        gat("Sc", SD, "c1u")
        tt("lt", CNT, "THR", OP.is_gt)
        mms([(SO, "lt", "RQ", True, False), (SO, "I16", "c1h", False, True)])
        mms([(X1P, "I16", X1, True, False), (X1P, "N16", FI, False, True)])
        tt("Sd", "Sc", X1P, OP.add)
        ts("Sn", "Sd", 2047, OP.bitwise_and)
        tt("so", SO, "IL", OP.min)
        ts("sou", "so", 2048.0, OP.add)
        sca(SD, "sou", "Sn")
        ts("n1", "si", 5, OP.mult, -16, OP.add)
        ts("h1", c1x, 0.0, OP.is_lt, 16777216.0, OP.mult)
        tt("h2", "h1", c1x, OP.add)
        tt("n2", "n1", u0, OP.add)
        ts("n3", "n2", 2047, OP.bitwise_and)
        tt("sb", "h2", "n3", OP.max)
        cp("x1", u1)
        listing(OO, "LK", "FS", 256, ("I16", "CT"))
        cp("ou", OO)
        act("z2", ZW, AF.Copy, off=("ou", 8, 16))
        act("z1", ZW, AF.Copy, off=("ou", 0, 8))
        mms([(XD, "BF2", SE, True, False), (XD, "IB", "xb", False, False), (XD, "NIB", "z2", False, True)])
        act("mX%d" % t, XD, AF.Abs, bias=1024.0)
        send(t, "mX%d" % t, "rX%d" % t, "aX%d" % t)
        ts("x2", "x1", 15, OP.bitwise_and)
        tt("x3", "x2", "XO", OP.add)
        cp("xou", "x3")
        sca(XW, "xou", "z1")
        mms([(XS, "BF1", FI, True, False), (XS, "IB", "xb", False, False), (XS, "IB", "z1", False, True)])
        act(X256, "xb", AF.Identity, bias=256.0)
        ts("xv", XS, 0.5, OP.mult, 2047.75, OP.add)
        tt(XBA, "xv", X256, OP.min)
        if last:
            dma("y", "oV", [XW], [], T.yv[:], T.ZX[:, 2048:4096], 2 * LOCAL)
            acc = ("b5", 0, 256)
            tt(acc, ("S", 0, 256), ("S", 256, 512), OP.add)
            for q in range(2, 8):
                tt(acc if q < 7 else "yto", acc, ("S", 256 * q, 256 * q + 256), OP.add)
            dma("y", "oT", ["yto"], [], T.yt[:], T.yto[:], LOCAL)
        tt("se", "sb", "rN%d" % t, OP.max)
        ts("si", "se", 2047, OP.bitwise_and)
        cp("sf" if last else "su", "si")
        if last:
            dma("s", "oS", ["sf"], [], T.ys[:], T.sf[:], LOCAL)
        tt("xm", XBA, "rX%d" % t, OP.min)
        ts("xn", "xm", 255, OP.bitwise_and)
        cp("xb", "xn")
    dma("y", "oX", ["xb"], [], T.yx[:], T.xb[:], LOCAL)
    return emit()
